import numpy as np
import ml_dtypes


def mxq(x, axis, fmt="e4m3"):
    dtype, down = {"e4m3": (ml_dtypes.float8_e4m3fn, 7), "e5m2": (ml_dtypes.float8_e5m2, 14)}[fmt]
    v = np.moveaxis(np.asarray(x, np.float32).astype(ml_dtypes.bfloat16).astype(np.float64), axis, -1)
    blocks = v.reshape(v.shape[:-1] + (-1, 32))
    amax = np.abs(blocks).max(-1, keepdims=True)
    byte = np.maximum(np.where(amax > 0, np.frexp(amax)[1] - 1 + 127, 0) - down, 1)
    scale = np.exp2(byte - 127.0)
    codes = (blocks / scale).astype(np.float32).astype(dtype).astype(np.float64)
    return np.moveaxis((codes * scale).reshape(v.shape), -1, axis)


WIDE = False


def mx_kscale(k):
    if not WIDE:
        return np.ones(k)
    levels = np.array([10, -10, 5, -5, 0])
    if k % 512:
        return np.exp2(np.random.permutation(np.resize(levels, k // 32))).repeat(32)
    a = np.empty((k // 512, 16))
    for p in range(k // 512):
        a[p, :8] = np.random.permutation(np.resize(levels, 8))
        for g in range(8):
            far = levels[np.abs(levels - a[p, g]) >= 10]
            a[p, g + 8] = far[np.random.randint(len(far))]
    return np.exp2(a.ravel()).repeat(32)


def f64(x):
    return np.asarray(x).astype(np.float64)


def striped(idx):
    return np.tile(idx.reshape(-1, 16).T, (8, 1)).astype(np.uint16)


def unstriped(offs):
    return offs[:16].T.reshape(-1).astype(np.int64)


def pack_weight(w):
    k, n = w.shape
    w = f64(np.asarray(w, np.float32).astype(ml_dtypes.bfloat16)).reshape(k // 32, 32, n)
    amax = np.abs(w).max(1)
    byte = np.clip(np.where(amax > 0, np.frexp(amax)[1] - 1 + 127 - 7, 1), 1, 254)
    scaled = (w * np.exp2(127.0 - byte)[:, None, :]).reshape(k, n).astype(np.float32)
    words = np.ascontiguousarray(scaled.reshape(k // 512, 128, 4, n).transpose(0, 1, 3, 2)).astype(ml_dtypes.float8_e4m3fn).view(np.uint8)
    return words, np.ascontiguousarray(byte.astype(np.uint8).reshape(k // 512, 16, n))


def unpack_weight(words, scales):
    g, p, n, _ = words.shape
    vals = np.ascontiguousarray(words).view(ml_dtypes.float8_e4m3fn).astype(np.float64) * np.repeat(np.exp2(scales.astype(np.float64) - 127.0), 8, axis=1)[..., None]
    return vals.transpose(0, 1, 3, 2).reshape(g * 512, n)


def sigmoid(v):
    return 1.0 / (1.0 + np.exp(-np.maximum(v, -700.0)))

def planes(y):
    n, m = y.shape
    v = y.astype(np.float32).astype(ml_dtypes.bfloat16).astype(np.float64).reshape(n // 32, 32, m)
    top = np.abs(v).max(1)
    byte = np.clip(np.where(top > 0, np.frexp(top)[1] - 1 + 127 - 7, 1), 1, 254)
    codes = (v * np.exp2(127.0 - byte)[:, None, :]).reshape(n, m).astype(np.float32).astype(ml_dtypes.float8_e4m3fn).view(np.uint8)
    words = codes.reshape(n // 512, 128, 4, m).transpose(0, 1, 3, 2)
    return np.ascontiguousarray(words), np.ascontiguousarray(byte.astype(np.uint8).reshape(n // 512, 16, m))


K, T, S, V, N = 512, 1024, 512, 256, 512


def setup_inputs():
    n = np.random.standard_normal
    s = mx_kscale(K)[:, None]
    packed_xT = pack_weight(n((K, T)) * s)
    return {
        "x_words": packed_xT[0],
        "x_scales": packed_xT[1],
        "w1": (n((K, N)) / np.sqrt(K) / s).astype(np.float32),
        "w2": (n((K, N)) / np.sqrt(K) / s).astype(np.float32),
        "w3": (n((K, N)) / np.sqrt(K) / s).astype(np.float32),
        "offs": striped(np.random.permutation(T)[:S]),
        "cen": striped(np.random.permutation(S)[:V]),
        "pos1": striped(np.random.permutation(S)[:V]),
        "pos2": striped(np.random.permutation(S)[:V]),
        "pos3": striped(np.random.permutation(S)[:V]),
    }


def reference(x_words, x_scales, w1, w2, w3, offs, cen, pos1, pos2, pos3):
    xq = unpack_weight(x_words, x_scales)[:, unstriped(offs)]
    y = mxq(f64(w1), 0, "e4m3").T @ xq
    yc = y[:, unstriped(cen)]
    e = mxq(f64(w2), 0, "e4m3").T @ xq
    h = mxq(f64(w3), 0, "e4m3").T @ xq
    z = (sigmoid(yc + e[:, unstriped(pos1)])) * h[:, unstriped(pos1)] + (sigmoid(yc + e[:, unstriped(pos2)])) * h[:, unstriped(pos2)] + (sigmoid(yc + e[:, unstriped(pos3)])) * h[:, unstriped(pos3)]
    out_0 = z
    return (out_0,) + planes(out_0)

@@ -1,0 +1,202 @@
+from contextlib import ExitStack
+
+import concourse.mybir as mybir
+
+K, T, S, V, N = 512, 1024, 512, 256, 512
+FLOPS = 3 * 2 * K * N * S
+
+F32 = mybir.dt.float32
+BF16 = mybir.dt.bfloat16
+I32 = mybir.dt.int32
+U32 = mybir.dt.uint32
+U16 = mybir.dt.uint16
+U8 = mybir.dt.uint8
+FP8X4 = mybir.dt.float8_e4m3fn_x4
+ADD = mybir.AluOpType.add
+MULT = mybir.AluOpType.mult
+SIGMOID = mybir.ActivationFunctionType.Sigmoid
+
+P = 128
+PACK = 4
+HALF = N // 2
+
+
+def tile_picked_gatedg_none_po_kernel(
+    tc, x_words, x_scales, w1, w2, w3, offs, cen, pos1, pos2, pos3, out_0, out_1, out_2
+):
+    nc = tc.nc
+    with ExitStack() as ctx:
+        lists = ctx.enter_context(tc.tile_pool(name="lists", bufs=1))
+        keep = ctx.enter_context(tc.tile_pool(name="keep", bufs=1))
+        psum = ctx.enter_context(tc.psum_pool(name="psum", bufs=8))
+
+        def load_list(name, src):
+            tile = lists.tile([P, src.shape[1]], U16, name=name)
+            nc.sync.dma_start(tile[:], src)
+            return tile
+
+        def load_half(name, w, half):
+            raw = keep.tile([P, PACK, HALF], F32, name=name)
+            cols = slice(half * HALF, (half + 1) * HALF)
+            nc.sync.dma_start(raw[:], w.rearrange("(p j) c -> p j c", j=PACK)[:, :, cols])
+            return raw
+
+        xs_all = keep.tile([P, T], U8, name="xs_all")
+        nc.vector.memset(xs_all[:].bitcast(I32), 0)
+        warm_in = keep.tile([P, 1], F32, name="warm_in")
+        warm_out = keep.tile([P, 1], F32, name="warm_out")
+        nc.gpsimd.memset(warm_in[:], 0.0)
+
+        offs_t = load_list("offs_t", offs)
+        xw_all = keep.tile([P, T], U32, name="xw_all")
+        nc.sync.dma_start(xw_all[:].bitcast(I32), x_words[0].rearrange("p n r -> p (n r)").bitcast(I32))
+        for q in range(4):
+            nc.scalar.dma_start(
+                xs_all[32 * q : 32 * q + 4, :].bitcast(I32), x_scales[0, 4 * q : 4 * q + 4, :].bitcast(I32)
+            )
+        nc.scalar.activation(warm_out[:], warm_in[:], SIGMOID)
+        raw = {}
+        raw["y", 0] = load_half("w1a", w1, 0)
+        raw["y", 1] = load_half("w1b", w1, 1)
+        cen_t = load_list("cen_t", cen)
+        raw["e", 0] = load_half("w2a", w2, 0)
+        raw["e", 1] = load_half("w2b", w2, 1)
+        pos_t = [load_list("pos%d_t" % d, src) for d, src in enumerate((pos1, pos2, pos3))]
+        raw["h", 0] = load_half("w3a", w3, 0)
+        raw["h", 1] = load_half("w3b", w3, 1)
+
+        xw = keep.tile([P, S], U32, name="xw", align_bytes=64)
+        xs = keep.tile([P, S], U8, name="xs", align_bytes=64)
+        nc.vector.tensor_copy(xw[:], xw_all[:].indirect(offs_t[:]))
+        nc.vector.tensor_copy(xs[:], xs_all[:].indirect(offs_t[:]))
+
+        grouped, codes, scales, rows = {}, {}, {}, {}
+        for name in ("y", "e", "h"):
+            grouped[name] = keep.tile([P, PACK, P, PACK], BF16, name="grouped_" + name, align_bytes=64)
+            codes[name] = keep.tile([P, N], U32, name="codes_" + name, align_bytes=64)
+            scales[name] = keep.tile([P, N], U8, name="scales_" + name, align_bytes=64)
+
+        def cast(name, half, copy):
+            ms = slice(half * P // 2, (half + 1) * P // 2)
+            copy(
+                grouped[name][:, :, ms, :].rearrange("p t m j -> p m j t"),
+                raw[name, half][:].rearrange("p j (m t) -> p m j t", t=PACK),
+            )
+
+        def quantise(name):
+            for t in range(PACK):
+                cols = slice(t * P, (t + 1) * P)
+                nc.vector.quantize_mx(
+                    out=codes[name][:, cols].bitcast(FP8X4),
+                    scales=scales[name][:, cols],
+                    in_=grouped[name][:, t, :, :].rearrange("p m j -> p (m j)"),
+                )
+
+        banks = {}
+
+        def product(name, t):
+            cols = slice(t * P, (t + 1) * P)
+            bank = psum.tile([P, S], F32, name="bank")
+            nc.tensor.matmul_mx(
+                out=bank[:],
+                lhsT=codes[name][:, cols].bitcast(FP8X4),
+                lhsT_scale=scales[name][:, cols],
+                rhs=xw[:].bitcast(FP8X4),
+                rhs_scale=xs[:],
+                start=True,
+                stop=True,
+            )
+            banks[name, t] = bank
+
+        def empty(name, t):
+            rows[name, t] = keep.tile([P, S], F32, name="rows_%s%d" % (name, t))
+            nc.scalar.copy(rows[name, t][:], banks[name, t][:])
+
+        yc, pre, gate = {}, {}, {}
+
+        def centre(t):
+            yc[t] = keep.tile([P, V], F32, name="yc%d" % t)
+            nc.vector.tensor_copy(yc[t][:], rows["y", t][:].indirect(cen_t[:]))
+
+        def both_ends(t):
+            pre[t] = keep.tile([P, 3, V], F32, name="pre%d" % t)
+            for d in range(3):
+                nc.vector.tensor_tensor(pre[t][:, d, :], rows["e", t][:].indirect(pos_t[d][:]), yc[t][:], ADD)
+
+        def squash(t):
+            gate[t] = keep.tile([P, 3, V], F32, name="gate%d" % t)
+            nc.scalar.activation(gate[t][:], pre[t][:], SIGMOID)
+
+        cast("y", 0, nc.scalar.copy)
+        cast("y", 1, nc.vector.tensor_copy)
+        quantise("y")
+        for t in range(PACK):
+            product("y", t)
+        cast("e", 0, nc.scalar.copy)
+        cast("e", 1, nc.vector.tensor_copy)
+        quantise("e")
+        for t in range(PACK):
+            product("e", t)
+        empty("y", 0)
+        empty("y", 1)
+        empty("y", 2)
+        empty("e", 0)
+        empty("y", 3)
+        empty("e", 1)
+        centre(0)
+        centre(1)
+        both_ends(0)
+        centre(2)
+        centre(3)
+        both_ends(1)
+        cast("h", 0, nc.scalar.copy)
+        cast("h", 1, nc.scalar.copy)
+        quantise("h")
+        for t in range(PACK):
+            product("h", t)
+        empty("e", 2)
+        empty("e", 3)
+        both_ends(2)
+        both_ends(3)
+        for t in range(PACK):
+            squash(t)
+            empty("h", t)
+
+        z = keep.tile([P, PACK, V], F32, name="z")
+        out_rows = out_0.rearrange("(p t) v -> p t v", t=PACK)
+        msg, part = {}, {}
+
+        def passed_on(t, d):
+            msg[t, d] = keep.tile([P, V], F32, name="msg%d_%d" % (t, d))
+            nc.vector.tensor_tensor(msg[t, d][:], rows["h", t][:].indirect(pos_t[d][:]), gate[t][:, d, :], MULT)
+
+        def finish(t):
+            nc.vector.tensor_tensor(z[:, t, :], part[t][:], msg[t, 2][:], ADD)
+            nc.sync.dma_start(out_rows[:, t, :], z[:, t, :])
+
+        for t in range(PACK):
+            passed_on(t, 0)
+            if t > 0:
+                finish(t - 1)
+            passed_on(t, 1)
+            passed_on(t, 2)
+            part[t] = keep.tile([P, V], F32, name="part%d" % t)
+            nc.vector.tensor_tensor(part[t][:], msg[t, 0][:], msg[t, 1][:], ADD)
+        finish(PACK - 1)
+
+        z_grouped = keep.tile([P, V, PACK], BF16, name="z_grouped", align_bytes=64)
+        nc.vector.tensor_copy(
+            z_grouped[:].rearrange("p (c i) t -> p c t i", i=4),
+            z[:].rearrange("p t (c i) -> p c t i", i=4),
+        )
+        z_codes = keep.tile([P, V], U32, name="z_codes", align_bytes=64)
+        z_scales = keep.tile([P, V], U8, name="z_scales", align_bytes=64)
+        nc.vector.quantize_mx(
+            out=z_codes[:].bitcast(FP8X4), scales=z_scales[:], in_=z_grouped[:].rearrange("p v t -> p (v t)")
+        )
+        nc.sync.dma_start(out_1[0].rearrange("p v r -> p (v r)").bitcast(I32), z_codes[:].bitcast(I32))
+        for q in range(4):
+            queue = nc.sync if q % 2 == 0 else nc.scalar
+            queue.dma_start(
+                out_2[0, 4 * q : 4 * q + 4, :].bitcast(I32), z_scales[32 * q : 32 * q + 4, :].bitcast(I32)
+            )

@@ -1,6 +1,7 @@
 from contextlib import ExitStack
 
 import concourse.mybir as mybir
+from concourse.masks import make_identity
 
 K, T, S, V, N = 512, 1024, 512, 256, 512
 FLOPS = 3 * 2 * K * N * S
@@ -28,7 +29,8 @@ def tile_picked_gatedg_none_po_kernel(
     with ExitStack() as ctx:
         lists = ctx.enter_context(tc.tile_pool(name="lists", bufs=1))
         keep = ctx.enter_context(tc.tile_pool(name="keep", bufs=1))
-        psum = ctx.enter_context(tc.psum_pool(name="psum", bufs=8))
+        psum = ctx.enter_context(tc.psum_pool(name="psum", bufs=5))
+        psum_sums = ctx.enter_context(tc.psum_pool(name="psum_sums", bufs=1))
 
         def load_list(name, src):
             tile = lists.tile([P, src.shape[1]], U16, name=name)
@@ -43,27 +45,26 @@ def tile_picked_gatedg_none_po_kernel(
 
         xs_all = keep.tile([P, T], U8, name="xs_all")
         nc.vector.memset(xs_all[:].bitcast(I32), 0)
-        warm_in = keep.tile([P, 1], F32, name="warm_in")
-        warm_out = keep.tile([P, 1], F32, name="warm_out")
-        nc.gpsimd.memset(warm_in[:], 0.0)
 
         offs_t = load_list("offs_t", offs)
         xw_all = keep.tile([P, T], U32, name="xw_all")
         nc.sync.dma_start(xw_all[:].bitcast(I32), x_words[0].rearrange("p n r -> p (n r)").bitcast(I32))
         for q in range(4):
-            nc.scalar.dma_start(
+            nc.sync.dma_start(
                 xs_all[32 * q : 32 * q + 4, :].bitcast(I32), x_scales[0, 4 * q : 4 * q + 4, :].bitcast(I32)
             )
-        nc.scalar.activation(warm_out[:], warm_in[:], SIGMOID)
         raw = {}
         raw["y", 0] = load_half("w1a", w1, 0)
         raw["y", 1] = load_half("w1b", w1, 1)
-        cen_t = load_list("cen_t", cen)
         raw["e", 0] = load_half("w2a", w2, 0)
         raw["e", 1] = load_half("w2b", w2, 1)
+        cen_t = load_list("cen_t", cen)
         pos_t = [load_list("pos%d_t" % d, src) for d, src in enumerate((pos1, pos2, pos3))]
         raw["h", 0] = load_half("w3a", w3, 0)
         raw["h", 1] = load_half("w3b", w3, 1)
+
+        identity = keep.tile([P, P], F32, name="identity")
+        make_identity(nc, identity[:])
 
         xw = keep.tile([P, S], U32, name="xw", align_bytes=64)
         xs = keep.tile([P, S], U8, name="xs", align_bytes=64)
@@ -83,13 +84,13 @@ def tile_picked_gatedg_none_po_kernel(
                 raw[name, half][:].rearrange("p j (m t) -> p m j t", t=PACK),
             )
 
-        def quantise(name):
-            for t in range(PACK):
-                cols = slice(t * P, (t + 1) * P)
+        def quantise(name, pieces):
+            for first, last in pieces:
+                cols = slice(first * P, last * P)
                 nc.vector.quantize_mx(
                     out=codes[name][:, cols].bitcast(FP8X4),
                     scales=scales[name][:, cols],
-                    in_=grouped[name][:, t, :, :].rearrange("p m j -> p (m j)"),
+                    in_=grouped[name][:, first:last, :, :].rearrange("p t m j -> p (t m j)"),
                 )
 
         banks = {}
@@ -108,8 +109,9 @@ def tile_picked_gatedg_none_po_kernel(
             )
             banks[name, t] = bank
 
-        def empty(name, t):
-            rows[name, t] = keep.tile([P, S], F32, name="rows_%s%d" % (name, t))
+        def empty(name, t, tag=None):
+            label = "rows_%s%d" % (name, t)
+            rows[name, t] = keep.tile([P, S], F32, name=label, tag=tag or label)
             nc.scalar.copy(rows[name, t][:], banks[name, t][:])
 
         yc, pre, gate = {}, {}, {}
@@ -124,39 +126,44 @@ def tile_picked_gatedg_none_po_kernel(
                 nc.vector.tensor_tensor(pre[t][:, d, :], rows["e", t][:].indirect(pos_t[d][:]), yc[t][:], ADD)
 
         def squash(t):
-            gate[t] = keep.tile([P, 3, V], F32, name="gate%d" % t)
+            if t == 0:
+                gate[t] = keep.tile([P, 3, V], F32, name="gate0", tag="w3a")
+            elif t == 1:
+                gate[t] = keep.tile([P, 3, V], F32, name="gate1", tag="grouped_h", align_bytes=64)
+            else:
+                gate[t] = keep.tile([P, 3, V], F32, name="gate%d" % t)
             nc.scalar.activation(gate[t][:], pre[t][:], SIGMOID)
 
         cast("y", 0, nc.scalar.copy)
         cast("y", 1, nc.vector.tensor_copy)
-        quantise("y")
+        quantise("y", ((0, 1), (1, 2), (2, 4)))
         for t in range(PACK):
             product("y", t)
+        empty("y", 0)
+        centre(0)
         cast("e", 0, nc.scalar.copy)
         cast("e", 1, nc.vector.tensor_copy)
-        quantise("e")
+        quantise("e", ((0, 4),))
         for t in range(PACK):
             product("e", t)
-        empty("y", 0)
         empty("y", 1)
         empty("y", 2)
-        empty("e", 0)
         empty("y", 3)
+        empty("e", 0)
         empty("e", 1)
-        centre(0)
+        empty("e", 2)
         centre(1)
-        both_ends(0)
         centre(2)
         centre(3)
+        both_ends(0)
         both_ends(1)
+        both_ends(2)
         cast("h", 0, nc.scalar.copy)
         cast("h", 1, nc.scalar.copy)
-        quantise("h")
+        quantise("h", ((0, 4),))
         for t in range(PACK):
             product("h", t)
-        empty("e", 2)
-        empty("e", 3)
-        both_ends(2)
+        empty("e", 3, "w3b")
         both_ends(3)
         for t in range(PACK):
             squash(t)
@@ -164,39 +171,90 @@ def tile_picked_gatedg_none_po_kernel(
 
         z = keep.tile([P, PACK, V], F32, name="z")
         out_rows = out_0.rearrange("(p t) v -> p t v", t=PACK)
-        msg, part = {}, {}
+        msg = {}
 
         def passed_on(t, d):
             msg[t, d] = keep.tile([P, V], F32, name="msg%d_%d" % (t, d))
             nc.vector.tensor_tensor(msg[t, d][:], rows["h", t][:].indirect(pos_t[d][:]), gate[t][:, d, :], MULT)
 
-        def finish(t):
-            nc.vector.tensor_tensor(z[:, t, :], part[t][:], msg[t, 2][:], ADD)
+        def sum_on_tensor(t):
+            turned = [psum_sums.tile([P, P], F32, name="turned%d" % half) for half in range(2)]
+            for d in range(3):
+                for half in range(2):
+                    nc.tensor.matmul(
+                        turned[half][:], msg[t, d][:, half * P : (half + 1) * P], identity[:],
+                        start=d == 0, stop=d == 2, is_transpose=True,
+                    )
+            held = keep.tile([P, 2, P], F32, name="held%d" % t)
+            back = psum_sums.tile([P, 2, P], F32, name="back")
+            for half in range(2):
+                nc.scalar.copy(held[:, half, :], turned[half][:])
+            for half in range(2):
+                nc.tensor.transpose(back[:, half, :], held[:, half, :], identity[:])
+            nc.scalar.copy(z[:, t, :], back[:].rearrange("p h v -> p (h v)"))
+
+        for t in range(PACK - 1):
+            for d in range(3):
+                passed_on(t, d)
+            sum_on_tensor(t)
             nc.sync.dma_start(out_rows[:, t, :], z[:, t, :])
 
-        for t in range(PACK):
-            passed_on(t, 0)
-            if t > 0:
-                finish(t - 1)
-            passed_on(t, 1)
-            passed_on(t, 2)
-            part[t] = keep.tile([P, V], F32, name="part%d" % t)
-            nc.vector.tensor_tensor(part[t][:], msg[t, 0][:], msg[t, 1][:], ADD)
-        finish(PACK - 1)
+        last = PACK - 1
+        HV = V // 2
+        halves = [slice(0, HV), slice(HV, V)]
+        tail = {}
 
-        z_grouped = keep.tile([P, V, PACK], BF16, name="z_grouped", align_bytes=64)
-        nc.vector.tensor_copy(
-            z_grouped[:].rearrange("p (c i) t -> p c t i", i=4),
-            z[:].rearrange("p t (c i) -> p c t i", i=4),
-        )
+        def passed_on_half(d, half):
+            tail[d, half] = keep.tile([P, HV], F32, name="tail%d_%d" % (d, half))
+            offsets = pos_t[d][:, half * HV // 16 : (half + 1) * HV // 16]
+            nc.vector.tensor_tensor(
+                tail[d, half][:], rows["h", last][:].indirect(offsets), gate[last][:, d, halves[half]], MULT
+            )
+
+        def first_add(half):
+            tail["part", half] = keep.tile([P, HV], F32, name="part%d" % half)
+            nc.vector.tensor_tensor(tail["part", half][:], tail[0, half][:], tail[1, half][:], ADD)
+
+        def second_add(half):
+            nc.vector.tensor_tensor(z[:, last, halves[half]], tail["part", half][:], tail[2, half][:], ADD)
+
+        z_grouped = {}
+
+        def group(half, copy):
+            z_grouped[half] = keep.tile([P, HV, PACK], BF16, name="z_grouped%d" % half, align_bytes=64)
+            copy(
+                z_grouped[half][:].rearrange("p (c i) t -> p c t i", i=4),
+                z[:, :, halves[half]].rearrange("p t (c i) -> p c t i", i=4),
+            )
+
         z_codes = keep.tile([P, V], U32, name="z_codes", align_bytes=64)
         z_scales = keep.tile([P, V], U8, name="z_scales", align_bytes=64)
-        nc.vector.quantize_mx(
-            out=z_codes[:].bitcast(FP8X4), scales=z_scales[:], in_=z_grouped[:].rearrange("p v t -> p (v t)")
-        )
-        nc.sync.dma_start(out_1[0].rearrange("p v r -> p (v r)").bitcast(I32), z_codes[:].bitcast(I32))
+        words_out = out_1[0].rearrange("p v r -> p (v r)").bitcast(I32)
+
+        def hand_on(half):
+            nc.vector.quantize_mx(
+                out=z_codes[:, halves[half]].bitcast(FP8X4),
+                scales=z_scales[:, halves[half]],
+                in_=z_grouped[half][:].rearrange("p v t -> p (v t)"),
+            )
+
+        for d in range(3):
+            passed_on_half(d, 0)
+        first_add(0)
+        passed_on_half(0, 1)
+        second_add(0)
+        group(0, nc.scalar.copy)
+        passed_on_half(1, 1)
+        passed_on_half(2, 1)
+        first_add(1)
+        hand_on(0)
+        second_add(1)
+        nc.sync.dma_start(out_rows[:, last, :], z[:, last, :])
+        group(1, nc.vector.tensor_copy)
+        hand_on(1)
+        nc.sync.dma_start(words_out, z_codes[:].bitcast(I32))
         for q in range(4):
-            queue = nc.sync if q % 2 == 0 else nc.scalar
+            queue = nc.sync if q % 2 == 1 else nc.scalar
             queue.dma_start(
                 out_2[0, 4 * q : 4 * q + 4, :].bitcast(I32), z_scales[32 * q : 32 * q + 4, :].bitcast(I32)
             )

@@ -29,8 +29,16 @@ def tile_picked_gatedg_none_po_kernel(
     with ExitStack() as ctx:
         lists = ctx.enter_context(tc.tile_pool(name="lists", bufs=1))
         keep = ctx.enter_context(tc.tile_pool(name="keep", bufs=1))
+        late = ctx.enter_context(tc.tile_pool(name="late", bufs=1))
         psum = ctx.enter_context(tc.psum_pool(name="psum", bufs=5))
         psum_sums = ctx.enter_context(tc.psum_pool(name="psum_sums", bufs=1))
+
+        reused = {"w2b":0,"rows_y3":0,"pre0_2":2048,"w3b":4096,"rows_e3":4096}
+
+        def place(shape, label, tag=None):
+            if label in reused:
+                return late.tile(shape, F32, name=label, offset=reused[label])
+            return keep.tile(shape, F32, name=label, tag=tag or label, align_bytes=64)
 
         def load_list(name, src):
             tile = lists.tile([P, src.shape[1]], U16, name=name)
@@ -38,27 +46,37 @@ def tile_picked_gatedg_none_po_kernel(
             return tile
 
         def load_half(name, w, half):
-            raw = keep.tile([P, PACK, HALF], F32, name=name)
+            raw = place([P, PACK, HALF], name)
             cols = slice(half * HALF, (half + 1) * HALF)
             nc.sync.dma_start(raw[:], w.rearrange("(p j) c -> p j c", j=PACK)[:, :, cols])
             return raw
 
         xs_all = keep.tile([P, T], U8, name="xs_all")
-        nc.vector.memset(xs_all[:].bitcast(I32), 0)
-
-        offs_t = load_list("offs_t", offs)
+        nc.gpsimd.memset(xs_all[:].bitcast(I32), 0)
         xw_all = keep.tile([P, T], U32, name="xw_all")
-        nc.sync.dma_start(xw_all[:].bitcast(I32), x_words[0].rearrange("p n r -> p (n r)").bitcast(I32))
-        for q in range(4):
-            nc.sync.dma_start(
-                xs_all[32 * q : 32 * q + 4, :].bitcast(I32), x_scales[0, 4 * q : 4 * q + 4, :].bitcast(I32)
-            )
+
+        def load_words():
+            nc.sync.dma_start(xw_all[:].bitcast(I32), x_words[0].rearrange("p n r -> p (n r)").bitcast(I32))
+
+        def load_scales(queue):
+            for q in range(4):
+                queue.dma_start(
+                    xs_all[32 * q : 32 * q + 4, :].bitcast(I32), x_scales[0, 4 * q : 4 * q + 4, :].bitcast(I32)
+                )
+
         raw = {}
+        warm_in = keep.tile([P, 1], F32, name="warm_in")
+        warm_out = keep.tile([P, 1], F32, name="warm_out")
+        nc.vector.memset(warm_in[:], 0.0)
+        nc.scalar.activation(warm_out[:], warm_in[:], SIGMOID)
+        offs_t = load_list("offs_t", offs)
+        load_scales(nc.sync)
+        load_words()
         raw["y", 0] = load_half("w1a", w1, 0)
         raw["y", 1] = load_half("w1b", w1, 1)
         raw["e", 0] = load_half("w2a", w2, 0)
-        raw["e", 1] = load_half("w2b", w2, 1)
         cen_t = load_list("cen_t", cen)
+        raw["e", 1] = load_half("w2b", w2, 1)
         pos_t = [load_list("pos%d_t" % d, src) for d, src in enumerate((pos1, pos2, pos3))]
         raw["h", 0] = load_half("w3a", w3, 0)
         raw["h", 1] = load_half("w3b", w3, 1)
@@ -68,40 +86,77 @@ def tile_picked_gatedg_none_po_kernel(
 
         xw = keep.tile([P, S], U32, name="xw", align_bytes=64)
         xs = keep.tile([P, S], U8, name="xs", align_bytes=64)
-        nc.vector.tensor_copy(xw[:], xw_all[:].indirect(offs_t[:]))
-        nc.vector.tensor_copy(xs[:], xs_all[:].indirect(offs_t[:]))
 
+        L = P // 2
         grouped, codes, scales, rows = {}, {}, {}, {}
-        for name in ("y", "e", "h"):
-            grouped[name] = keep.tile([P, PACK, P, PACK], BF16, name="grouped_" + name, align_bytes=64)
-            codes[name] = keep.tile([P, N], U32, name="codes_" + name, align_bytes=64)
-            scales[name] = keep.tile([P, N], U8, name="scales_" + name, align_bytes=64)
 
-        def cast(name, half, copy):
-            ms = slice(half * P // 2, (half + 1) * P // 2)
+        def operand(name, block):
+            if (name, block) not in codes:
+                label = "%s%d" % (name, block)
+                codes[name, block] = keep.tile([P, P], U32, name="codes_" + label, align_bytes=64)
+                scales[name, block] = keep.tile([P, P], U8, name="scales_" + label, align_bytes=64)
+            return codes[name, block], scales[name, block]
+
+        def cast(name, half, first, last, copy):
+            if (name, half) not in grouped:
+                label = "grouped_%s%d" % (name, half)
+                grouped[name, half] = keep.tile([P, PACK, L, PACK], BF16, name=label, align_bytes=64)
             copy(
-                grouped[name][:, :, ms, :].rearrange("p t m j -> p m j t"),
-                raw[name, half][:].rearrange("p j (m t) -> p m j t", t=PACK),
+                grouped[name, half][:, first:last].rearrange("p t l j -> p l j t"),
+                raw[name, half][:].rearrange("p j (l t) -> p l j t", t=PACK)[:, :, :, first:last],
             )
 
-        def quantise(name, pieces):
-            for first, last in pieces:
-                cols = slice(first * P, last * P)
+        def quantise(name, half, pair):
+            if pair == 0:
+                words, plane = operand(name, half)
                 nc.vector.quantize_mx(
-                    out=codes[name][:, cols].bitcast(FP8X4),
-                    scales=scales[name][:, cols],
-                    in_=grouped[name][:, first:last, :, :].rearrange("p t m j -> p (t m j)"),
+                    out=words[:].bitcast(FP8X4),
+                    scales=plane[:],
+                    in_=grouped[name, half][:, 0:2].rearrange("p u l j -> p (u l j)"),
                 )
+            else:
+                cols = slice(half * L, (half + 1) * L)
+                for u in range(2):
+                    words, plane = operand(name, 2 + u)
+                    nc.vector.quantize_mx(
+                        out=words[:, cols].bitcast(FP8X4),
+                        scales=plane[:, cols],
+                        in_=grouped[name, half][:, 2 + u].rearrange("p l j -> p (l j)"),
+                    )
+
+        grouped_h = keep.tile([P, PACK, 2, L, PACK], BF16, name="grouped_h", align_bytes=64)
+        codes_h = keep.tile([P, N], U32, name="codes_h", align_bytes=64)
+        scales_h = keep.tile([P, N], U8, name="scales_h", align_bytes=64)
+
+        def cast_h(half, pair):
+            if pair == 0:
+                dst = grouped_h[:, half, :, :, :]
+            else:
+                dst = grouped_h[:, 2:4, half, :, :]
+            nc.scalar.copy(
+                dst.rearrange("p u l j -> p l j u"),
+                raw["h", half][:].rearrange("p j (l t) -> p l j t", t=PACK)[:, :, :, 2 * pair : 2 * pair + 2],
+            )
+
+        def quantise_h(first, last):
+            cols = slice(first * P, last * P)
+            nc.vector.quantize_mx(
+                out=codes_h[:, cols].bitcast(FP8X4),
+                scales=scales_h[:, cols],
+                in_=grouped_h[:, first:last].rearrange("p a b l j -> p (a b l j)"),
+            )
+            for block in range(first, last):
+                codes["h", block] = codes_h[:, block * P : (block + 1) * P]
+                scales["h", block] = scales_h[:, block * P : (block + 1) * P]
 
         banks = {}
 
         def product(name, t):
-            cols = slice(t * P, (t + 1) * P)
             bank = psum.tile([P, S], F32, name="bank")
             nc.tensor.matmul_mx(
                 out=bank[:],
-                lhsT=codes[name][:, cols].bitcast(FP8X4),
-                lhsT_scale=scales[name][:, cols],
+                lhsT=codes[name, t][:].bitcast(FP8X4),
+                lhsT_scale=scales[name, t][:],
                 rhs=xw[:].bitcast(FP8X4),
                 rhs_scale=xs[:],
                 start=True,
@@ -111,93 +166,147 @@ def tile_picked_gatedg_none_po_kernel(
 
         def empty(name, t, tag=None):
             label = "rows_%s%d" % (name, t)
-            rows[name, t] = keep.tile([P, S], F32, name=label, tag=tag or label)
+            rows[name, t] = place([P, S], label, tag)
             nc.scalar.copy(rows[name, t][:], banks[name, t][:])
 
         yc, pre, gate = {}, {}, {}
 
-        def centre(t):
-            yc[t] = keep.tile([P, V], F32, name="yc%d" % t)
+        def centre(t, tag=None):
+            if t == 0:
+                yc["all"] = keep.tile([P, PACK, V], F32, name="centres", tag="w2a", align_bytes=64)
+            yc[t] = yc["all"][:, t, :]
             nc.vector.tensor_copy(yc[t][:], rows["y", t][:].indirect(cen_t[:]))
 
-        def both_ends(t):
-            pre[t] = keep.tile([P, 3, V], F32, name="pre%d" % t)
-            for d in range(3):
-                nc.vector.tensor_tensor(pre[t][:, d, :], rows["e", t][:].indirect(pos_t[d][:]), yc[t][:], ADD)
+        def both_ends(t, first=0, last=3, tag=None):
+            label = "pre%d_%d" % (t, first)
+            part = place([P, last - first, V], label, tag)
+            pre.setdefault(t, []).append((first, last, part))
+            for d in range(first, last):
+                nc.vector.tensor_tensor(part[:, d - first, :], rows["e", t][:].indirect(pos_t[d][:]), yc[t][:], ADD)
 
         def squash(t):
             if t == 0:
-                gate[t] = keep.tile([P, 3, V], F32, name="gate0", tag="w3a")
-            elif t == 1:
-                gate[t] = keep.tile([P, 3, V], F32, name="gate1", tag="grouped_h", align_bytes=64)
-            else:
-                gate[t] = keep.tile([P, 3, V], F32, name="gate%d" % t)
-            nc.scalar.activation(gate[t][:], pre[t][:], SIGMOID)
-
-        cast("y", 0, nc.scalar.copy)
-        cast("y", 1, nc.vector.tensor_copy)
-        quantise("y", ((0, 1), (1, 2), (2, 4)))
-        for t in range(PACK):
-            product("y", t)
-        empty("y", 0)
-        centre(0)
-        cast("e", 0, nc.scalar.copy)
-        cast("e", 1, nc.vector.tensor_copy)
-        quantise("e", ((0, 4),))
-        for t in range(PACK):
-            product("e", t)
-        empty("y", 1)
-        empty("y", 2)
-        empty("y", 3)
-        empty("e", 0)
-        empty("e", 1)
-        empty("e", 2)
-        centre(1)
-        centre(2)
-        centre(3)
-        both_ends(0)
-        both_ends(1)
-        both_ends(2)
-        cast("h", 0, nc.scalar.copy)
-        cast("h", 1, nc.scalar.copy)
-        quantise("h", ((0, 4),))
-        for t in range(PACK):
-            product("h", t)
-        empty("e", 3, "w3b")
-        both_ends(3)
-        for t in range(PACK):
-            squash(t)
-            empty("h", t)
+                gate["all"] = place([P, PACK, 3, V], "gates", "w3a")
+            gate[t] = gate["all"][:, t]
+            for first, last, part in pre[t]:
+                nc.scalar.activation(gate[t][:, first:last, :], part[:], SIGMOID)
 
         z = keep.tile([P, PACK, V], F32, name="z")
         out_rows = out_0.rearrange("(p t) v -> p t v", t=PACK)
-        msg = {}
+        msg, turned = {}, {}
+        held01 = keep.tile([P, 2, 2, P], F32, name="held01")
+        held2 = keep.tile([P, 2, P], F32, name="held2")
 
-        def passed_on(t, d):
-            msg[t, d] = keep.tile([P, V], F32, name="msg%d_%d" % (t, d))
-            nc.vector.tensor_tensor(msg[t, d][:], rows["h", t][:].indirect(pos_t[d][:]), gate[t][:, d, :], MULT)
+        def passed_on(t):
+            for d in range(3):
+                msg[t, d] = keep.tile([P, V], F32, name="msg%d_%d" % (t, d))
+                nc.vector.tensor_tensor(msg[t, d][:], rows["h", t][:].indirect(pos_t[d][:]), gate[t][:, d, :], MULT)
 
-        def sum_on_tensor(t):
-            turned = [psum_sums.tile([P, P], F32, name="turned%d" % half) for half in range(2)]
+        def turn(t):
+            for half in range(2):
+                turned[t, half] = psum_sums.tile([P, P], F32, name="turned%d" % half)
             for d in range(3):
                 for half in range(2):
                     nc.tensor.matmul(
-                        turned[half][:], msg[t, d][:, half * P : (half + 1) * P], identity[:],
+                        turned[t, half][:], msg[t, d][:, half * P : (half + 1) * P], identity[:],
                         start=d == 0, stop=d == 2, is_transpose=True,
                     )
-            held = keep.tile([P, 2, P], F32, name="held%d" % t)
+
+        def hold(t):
+            for half in range(2):
+                if t < 2:
+                    nc.scalar.copy(
+                        held01[:, half, :, t * L : (t + 1) * L], turned[t, half][:].rearrange("v (u l) -> v u l", u=2)
+                    )
+                else:
+                    nc.scalar.copy(held2[:, half, :], turned[t, half][:])
+
+        def back01():
+            back = psum_sums.tile([P, 2, 2, P], F32, name="back")
+            for u in range(2):
+                for half in range(2):
+                    nc.tensor.transpose(back[:, u, half, :], held01[:, half, u, :], identity[:])
+            nc.scalar.copy(z[:, 0:2, :], back[:].rearrange("p u h v -> p u (h v)"))
+            nc.sync.dma_start(out_rows[:, 0:2, :], z[:, 0:2, :])
+
+        def back2():
             back = psum_sums.tile([P, 2, P], F32, name="back")
             for half in range(2):
-                nc.scalar.copy(held[:, half, :], turned[half][:])
-            for half in range(2):
-                nc.tensor.transpose(back[:, half, :], held[:, half, :], identity[:])
-            nc.scalar.copy(z[:, t, :], back[:].rearrange("p h v -> p (h v)"))
+                nc.tensor.transpose(back[:, half, :], held2[:, half, :], identity[:])
+            nc.scalar.copy(z[:, 2, :], back[:].rearrange("p h v -> p (h v)"))
+            nc.sync.dma_start(out_rows[:, 2, :], z[:, 2, :])
 
-        for t in range(PACK - 1):
-            for d in range(3):
-                passed_on(t, d)
-            sum_on_tensor(t)
-            nc.sync.dma_start(out_rows[:, t, :], z[:, t, :])
+        on_scalar, on_vector = nc.scalar.copy, nc.vector.tensor_copy
+        nc.vector.tensor_copy(xs[:], xs_all[:].indirect(offs_t[:]))
+        nc.vector.tensor_copy(xw[:], xw_all[:].indirect(offs_t[:]))
+        cast("y", 0, 0, 2, on_vector)
+        quantise("y", 0, 0)
+        product("y", 0)
+        cast("y", 0, 2, 4, on_scalar)
+        quantise("y", 0, 1)
+        cast("y", 1, 0, 2, on_vector)
+        cast("y", 1, 2, 4, on_scalar)
+        quantise("y", 1, 0)
+        product("y", 1)
+        empty("y", 0, "w1b")
+        cast("e", 0, 0, 4, on_vector)
+        centre(0, "w2a")
+        quantise("y", 1, 1)
+        product("y", 2)
+        product("y", 3)
+        quantise("e", 0, 0)
+        product("e", 0)
+        quantise("e", 0, 1)
+        empty("y", 1)
+        empty("y", 2)
+        empty("e", 0)
+        centre(1)
+        centre(2)
+        cast("e", 1, 0, 2, on_scalar)
+        cast("e", 1, 2, 4, on_scalar)
+        both_ends(0, 0, 2)
+        quantise("e", 1, 0)
+        product("e", 1)
+        quantise("e", 1, 1)
+        product("e", 2)
+        product("e", 3)
+        both_ends(0, 2, 3)
+        empty("y", 3)
+        centre(3)
+        empty("e", 1)
+        both_ends(1)
+        cast_h(0, 0)
+        empty("e", 2)
+        cast_h(1, 0)
+        cast_h(0, 1)
+        cast_h(1, 1)
+        empty("e", 3)
+        both_ends(2)
+        quantise_h(0, 4)
+        product("h", 0)
+        product("h", 1)
+        product("h", 2)
+        product("h", 3)
+        both_ends(3)
+        squash(0)
+        empty("h", 0)
+        passed_on(0)
+        squash(1)
+        empty("h", 1)
+        passed_on(1)
+        squash(2)
+        empty("h", 2)
+        passed_on(2)
+        squash(3)
+        empty("h", 3)
+        turn(0)
+        hold(0)
+        turn(1)
+        hold(1)
+        back01()
+        turn(2)
+        hold(2)
+        back2()
 
         last = PACK - 1
         HV = V // 2

@@ -230,10 +230,10 @@ def tile_picked_gatedg_none_po_kernel(
             nc.sync.dma_start(out_rows[:, 0:2, :], z[:, 0:2, :])
 
         def back2():
-            back = psum_sums.tile([P, 2, P], F32, name="back")
             for half in range(2):
-                nc.tensor.transpose(back[:, half, :], held2[:, half, :], identity[:])
-            nc.scalar.copy(z[:, 2, :], back[:].rearrange("p h v -> p (h v)"))
+                back = psum.tile([P, P], F32, name="bank")
+                nc.tensor.transpose(back[:], held2[:, half, :], identity[:])
+                nc.scalar.copy(z[:, 2, half * P : (half + 1) * P], back[:])
             nc.sync.dma_start(out_rows[:, 2, :], z[:, 2, :])
 
         on_scalar, on_vector = nc.scalar.copy, nc.vector.tensor_copy
@@ -289,18 +289,18 @@ def tile_picked_gatedg_none_po_kernel(
         product("h", 3)
         both_ends(3)
         squash(0)
+        squash(1)
         empty("h", 0)
         passed_on(0)
-        squash(1)
+        squash(2)
         empty("h", 1)
         passed_on(1)
-        squash(2)
         empty("h", 2)
         passed_on(2)
         squash(3)
-        empty("h", 3)
         turn(0)
         hold(0)
+        empty("h", 3)
         turn(1)
         hold(1)
         back01()

@@ -33,7 +33,7 @@ def tile_picked_gatedg_none_po_kernel(
         psum = ctx.enter_context(tc.psum_pool(name="psum", bufs=5))
         psum_sums = ctx.enter_context(tc.psum_pool(name="psum_sums", bufs=1))
 
-        reused = {"w2b":0,"rows_y3":0,"pre0_2":2048,"w3b":4096,"rows_e3":4096}
+        reused = {}
 
         def place(shape, label, tag=None):
             if label in reused:
@@ -73,8 +73,8 @@ def tile_picked_gatedg_none_po_kernel(
         load_scales(nc.sync)
         load_words()
         raw["y", 0] = load_half("w1a", w1, 0)
-        raw["y", 1] = load_half("w1b", w1, 1)
         raw["e", 0] = load_half("w2a", w2, 0)
+        raw["y", 1] = load_half("w1b", w1, 1)
         cen_t = load_list("cen_t", cen)
         raw["e", 1] = load_half("w2b", w2, 1)
         pos_t = [load_list("pos%d_t" % d, src) for d, src in enumerate((pos1, pos2, pos3))]
@@ -166,14 +166,21 @@ def tile_picked_gatedg_none_po_kernel(
 
         def empty(name, t, tag=None):
             label = "rows_%s%d" % (name, t)
-            rows[name, t] = place([P, S], label, tag)
+            if name == "y" and t > 0:
+                if t == 1:
+                    rows["y", "rest"] = keep.tile([P, 3, S], F32, name="rows_y_rest", tag="w2b", align_bytes=64)
+                rows[name, t] = rows["y", "rest"][:, t - 1, :]
+            elif label == "rows_e3":
+                rows[name, t] = keep.tile([P, S], F32, name=label, tag="w3b", align_bytes=64)
+            else:
+                rows[name, t] = place([P, S], label, tag)
             nc.scalar.copy(rows[name, t][:], banks[name, t][:])
 
         yc, pre, gate = {}, {}, {}
 
         def centre(t, tag=None):
             if t == 0:
-                yc["all"] = keep.tile([P, PACK, V], F32, name="centres", tag="w2a", align_bytes=64)
+                yc["all"] = keep.tile([P, PACK, V], F32, name="centres", align_bytes=64)
             yc[t] = yc["all"][:, t, :]
             nc.vector.tensor_copy(yc[t][:], rows["y", t][:].indirect(cen_t[:]))
 
@@ -244,36 +251,35 @@ def tile_picked_gatedg_none_po_kernel(
         product("y", 0)
         cast("y", 0, 2, 4, on_scalar)
         quantise("y", 0, 1)
-        cast("y", 1, 0, 2, on_vector)
-        cast("y", 1, 2, 4, on_scalar)
-        quantise("y", 1, 0)
-        product("y", 1)
-        empty("y", 0, "w1b")
-        cast("e", 0, 0, 4, on_vector)
-        centre(0, "w2a")
-        quantise("y", 1, 1)
-        product("y", 2)
-        product("y", 3)
+        cast("e", 0, 0, 2, on_vector)
+        cast("e", 0, 2, 4, on_scalar)
         quantise("e", 0, 0)
         product("e", 0)
         quantise("e", 0, 1)
-        empty("y", 1)
-        empty("y", 2)
+        empty("y", 0, "w2a")
         empty("e", 0)
-        centre(1)
-        centre(2)
+        cast("y", 1, 0, 4, on_vector)
+        centre(0)
+        quantise("y", 1, 0)
+        product("y", 1)
+        quantise("y", 1, 1)
+        product("y", 2)
+        product("y", 3)
         cast("e", 1, 0, 2, on_scalar)
         cast("e", 1, 2, 4, on_scalar)
-        both_ends(0, 0, 2)
+        both_ends(0)
         quantise("e", 1, 0)
         product("e", 1)
         quantise("e", 1, 1)
         product("e", 2)
         product("e", 3)
-        both_ends(0, 2, 3)
+        empty("y", 1)
+        empty("y", 2)
         empty("y", 3)
-        centre(3)
         empty("e", 1)
+        centre(1)
+        centre(2)
+        centre(3)
         both_ends(1)
         cast_h(0, 0)
         empty("e", 2)

@@ -58,8 +58,8 @@ def tile_picked_gatedg_none_po_kernel(
         def load_words():
             nc.sync.dma_start(xw_all[:].bitcast(I32), x_words[0].rearrange("p n r -> p (n r)").bitcast(I32))
 
-        def load_scales(queue):
-            for q in range(4):
+        def load_scales(queues):
+            for q, queue in enumerate(queues):
                 queue.dma_start(
                     xs_all[32 * q : 32 * q + 4, :].bitcast(I32), x_scales[0, 4 * q : 4 * q + 4, :].bitcast(I32)
                 )
@@ -67,10 +67,10 @@ def tile_picked_gatedg_none_po_kernel(
         raw = {}
         warm_in = keep.tile([P, 1], F32, name="warm_in")
         warm_out = keep.tile([P, 1], F32, name="warm_out")
-        nc.vector.memset(warm_in[:], 0.0)
-        nc.scalar.activation(warm_out[:], warm_in[:], SIGMOID)
+        nc.gpsimd.memset(warm_in[:], 0.0)
         offs_t = load_list("offs_t", offs)
-        load_scales(nc.sync)
+        load_scales((nc.scalar, nc.scalar, nc.sync, nc.sync))
+        nc.scalar.activation(warm_out[:], warm_in[:], SIGMOID)
         load_words()
         raw["y", 0] = load_half("w1a", w1, 0)
         raw["e", 0] = load_half("w2a", w2, 0)

@@ -33,7 +33,7 @@ def tile_picked_gatedg_none_po_kernel(
         psum = ctx.enter_context(tc.psum_pool(name="psum", bufs=5))
         psum_sums = ctx.enter_context(tc.psum_pool(name="psum_sums", bufs=1))
 
-        reused = {}
+        reused = {"rows_e3": 0, "w3": 1024, "gates": 2048}
 
         def place(shape, label, tag=None):
             if label in reused:
@@ -55,8 +55,10 @@ def tile_picked_gatedg_none_po_kernel(
         nc.gpsimd.memset(xs_all[:].bitcast(I32), 0)
         xw_all = keep.tile([P, T], U32, name="xw_all")
 
-        def load_words():
-            nc.sync.dma_start(xw_all[:].bitcast(I32), x_words[0].rearrange("p n r -> p (n r)").bitcast(I32))
+        def load_words(half):
+            cols = slice(half * T // 2, (half + 1) * T // 2)
+            words_in = x_words[0].rearrange("p n r -> p (n r)").bitcast(I32)
+            nc.sync.dma_start(xw_all[:, cols].bitcast(I32), words_in[:, cols])
 
         def load_scales(queues):
             for q, queue in enumerate(queues):
@@ -69,17 +71,20 @@ def tile_picked_gatedg_none_po_kernel(
         warm_out = keep.tile([P, 1], F32, name="warm_out")
         nc.gpsimd.memset(warm_in[:], 0.0)
         offs_t = load_list("offs_t", offs)
+        load_words(0)
         load_scales((nc.scalar, nc.scalar, nc.sync, nc.sync))
         nc.scalar.activation(warm_out[:], warm_in[:], SIGMOID)
-        load_words()
+        load_words(1)
         raw["y", 0] = load_half("w1a", w1, 0)
         raw["e", 0] = load_half("w2a", w2, 0)
         raw["y", 1] = load_half("w1b", w1, 1)
         cen_t = load_list("cen_t", cen)
         raw["e", 1] = load_half("w2b", w2, 1)
         pos_t = [load_list("pos%d_t" % d, src) for d, src in enumerate((pos1, pos2, pos3))]
-        raw["h", 0] = load_half("w3a", w3, 0)
-        raw["h", 1] = load_half("w3b", w3, 1)
+        raw_h = place([P, PACK, N], "w3")
+        nc.sync.dma_start(raw_h[:], w3.rearrange("(p j) c -> p j c", j=PACK))
+        for half in range(2):
+            raw["h", half] = raw_h[:, :, half * HALF : (half + 1) * HALF]
 
         identity = keep.tile([P, P], F32, name="identity")
         make_identity(nc, identity[:])
@@ -170,8 +175,6 @@ def tile_picked_gatedg_none_po_kernel(
                 if t == 1:
                     rows["y", "rest"] = keep.tile([P, 3, S], F32, name="rows_y_rest", tag="w2b", align_bytes=64)
                 rows[name, t] = rows["y", "rest"][:, t - 1, :]
-            elif label == "rows_e3":
-                rows[name, t] = keep.tile([P, S], F32, name=label, tag="w3b", align_bytes=64)
             else:
                 rows[name, t] = place([P, S], label, tag)
             nc.scalar.copy(rows[name, t][:], banks[name, t][:])
@@ -193,7 +196,7 @@ def tile_picked_gatedg_none_po_kernel(
 
         def squash(t):
             if t == 0:
-                gate["all"] = place([P, PACK, 3, V], "gates", "w3a")
+                gate["all"] = place([P, PACK, 3, V], "gates")
             gate[t] = gate["all"][:, t]
             for first, last, part in pre[t]:
                 nc.scalar.activation(gate[t][:, first:last, :], part[:], SIGMOID)
@@ -246,7 +249,7 @@ def tile_picked_gatedg_none_po_kernel(
         on_scalar, on_vector = nc.scalar.copy, nc.vector.tensor_copy
         nc.vector.tensor_copy(xs[:], xs_all[:].indirect(offs_t[:]))
         nc.vector.tensor_copy(xw[:], xw_all[:].indirect(offs_t[:]))
-        cast("y", 0, 0, 2, on_vector)
+        cast("y", 0, 0, 2, on_scalar)
         quantise("y", 0, 0)
         product("y", 0)
         cast("y", 0, 2, 4, on_scalar)

@@ -20,6 +20,7 @@ SIGMOID = mybir.ActivationFunctionType.Sigmoid
 P = 128
 PACK = 4
 HALF = N // 2
+EARLY = T // 2
 
 
 def tile_picked_gatedg_none_po_kernel(
@@ -55,8 +56,7 @@ def tile_picked_gatedg_none_po_kernel(
         nc.gpsimd.memset(xs_all[:].bitcast(I32), 0)
         xw_all = keep.tile([P, T], U32, name="xw_all")
 
-        def load_words(half):
-            cols = slice(half * T // 2, (half + 1) * T // 2)
+        def load_words(cols):
             words_in = x_words[0].rearrange("p n r -> p (n r)").bitcast(I32)
             nc.sync.dma_start(xw_all[:, cols].bitcast(I32), words_in[:, cols])
 
@@ -70,11 +70,11 @@ def tile_picked_gatedg_none_po_kernel(
         warm_in = keep.tile([P, 1], F32, name="warm_in")
         warm_out = keep.tile([P, 1], F32, name="warm_out")
         nc.gpsimd.memset(warm_in[:], 0.0)
+        load_words(slice(0, EARLY))
         offs_t = load_list("offs_t", offs)
-        load_words(0)
         load_scales((nc.scalar, nc.scalar, nc.sync, nc.sync))
         nc.scalar.activation(warm_out[:], warm_in[:], SIGMOID)
-        load_words(1)
+        load_words(slice(EARLY, T))
         raw["y", 0] = load_half("w1a", w1, 0)
         raw["e", 0] = load_half("w2a", w2, 0)
         raw["y", 1] = load_half("w1b", w1, 1)
@@ -207,8 +207,8 @@ def tile_picked_gatedg_none_po_kernel(
         held01 = keep.tile([P, 2, 2, P], F32, name="held01")
         held2 = keep.tile([P, 2, P], F32, name="held2")
 
-        def passed_on(t):
-            for d in range(3):
+        def passed_on(t, count=3):
+            for d in range(count):
                 msg[t, d] = keep.tile([P, V], F32, name="msg%d_%d" % (t, d))
                 nc.vector.tensor_tensor(msg[t, d][:], rows["h", t][:].indirect(pos_t[d][:]), gate[t][:, d, :], MULT)
 
@@ -329,12 +329,12 @@ def tile_picked_gatedg_none_po_kernel(
                 tail[d, half][:], rows["h", last][:].indirect(offsets), gate[last][:, d, halves[half]], MULT
             )
 
-        def first_add(half):
-            tail["part", half] = keep.tile([P, HV], F32, name="part%d" % half)
-            nc.vector.tensor_tensor(tail["part", half][:], tail[0, half][:], tail[1, half][:], ADD)
+        def first_add():
+            tail["part"] = keep.tile([P, V], F32, name="part")
+            nc.vector.tensor_tensor(tail["part"][:], msg[last, 0][:], msg[last, 1][:], ADD)
 
         def second_add(half):
-            nc.vector.tensor_tensor(z[:, last, halves[half]], tail["part", half][:], tail[2, half][:], ADD)
+            nc.vector.tensor_tensor(z[:, last, halves[half]], tail["part"][:, halves[half]], tail[2, half][:], ADD)
 
         z_grouped = {}
 
@@ -356,19 +356,16 @@ def tile_picked_gatedg_none_po_kernel(
                 in_=z_grouped[half][:].rearrange("p v t -> p (v t)"),
             )
 
-        for d in range(3):
-            passed_on_half(d, 0)
-        first_add(0)
-        passed_on_half(0, 1)
+        passed_on(last, 2)
+        passed_on_half(2, 0)
+        first_add()
+        passed_on_half(2, 1)
         second_add(0)
         group(0, nc.scalar.copy)
-        passed_on_half(1, 1)
-        passed_on_half(2, 1)
-        first_add(1)
-        hand_on(0)
         second_add(1)
         nc.sync.dma_start(out_rows[:, last, :], z[:, last, :])
         group(1, nc.vector.tensor_copy)
+        hand_on(0)
         hand_on(1)
         nc.sync.dma_start(words_out, z_codes[:].bitcast(I32))
         for q in range(4):

@@ -34,7 +34,7 @@ def tile_picked_gatedg_none_po_kernel(
         psum = ctx.enter_context(tc.psum_pool(name="psum", bufs=5))
         psum_sums = ctx.enter_context(tc.psum_pool(name="psum_sums", bufs=1))
 
-        reused = {"rows_e3": 0, "w3": 1024, "gates": 2048}
+        reused = {"rows_e3": 0, "w3": 1024, "rows_h0": 2048, "rows_h1": 4096, "gates": 6144}
 
         def place(shape, label, tag=None):
             if label in reused:
@@ -79,8 +79,9 @@ def tile_picked_gatedg_none_po_kernel(
         raw["e", 0] = load_half("w2a", w2, 0)
         raw["y", 1] = load_half("w1b", w1, 1)
         cen_t = load_list("cen_t", cen)
+        pos_t = [load_list("pos0_t", pos1)]
         raw["e", 1] = load_half("w2b", w2, 1)
-        pos_t = [load_list("pos%d_t" % d, src) for d, src in enumerate((pos1, pos2, pos3))]
+        pos_t.extend([load_list("pos1_t", pos2), load_list("pos2_t", pos3)])
         raw_h = place([P, PACK, N], "w3")
         nc.sync.dma_start(raw_h[:], w3.rearrange("(p j) c -> p j c", j=PACK))
         for half in range(2):
@@ -207,8 +208,8 @@ def tile_picked_gatedg_none_po_kernel(
         held01 = keep.tile([P, 2, 2, P], F32, name="held01")
         held2 = keep.tile([P, 2, P], F32, name="held2")
 
-        def passed_on(t, count=3):
-            for d in range(count):
+        def passed_on(t):
+            for d in range(3):
                 msg[t, d] = keep.tile([P, V], F32, name="msg%d_%d" % (t, d))
                 nc.vector.tensor_tensor(msg[t, d][:], rows["h", t][:].indirect(pos_t[d][:]), gate[t][:, d, :], MULT)
 
@@ -287,22 +288,23 @@ def tile_picked_gatedg_none_po_kernel(
         cast_h(0, 0)
         empty("e", 2)
         cast_h(1, 0)
+        quantise_h(0, 2)
+        product("h", 0)
+        product("h", 1)
         cast_h(0, 1)
         cast_h(1, 1)
         empty("e", 3)
         both_ends(2)
-        quantise_h(0, 4)
-        product("h", 0)
-        product("h", 1)
+        quantise_h(2, 4)
         product("h", 2)
         product("h", 3)
         both_ends(3)
         squash(0)
-        squash(1)
         empty("h", 0)
+        squash(1)
         passed_on(0)
-        squash(2)
         empty("h", 1)
+        squash(2)
         passed_on(1)
         empty("h", 2)
         passed_on(2)
@@ -320,21 +322,15 @@ def tile_picked_gatedg_none_po_kernel(
         last = PACK - 1
         HV = V // 2
         halves = [slice(0, HV), slice(HV, V)]
-        tail = {}
+        part = keep.tile([P, V], F32, name="part")
 
-        def passed_on_half(d, half):
-            tail[d, half] = keep.tile([P, HV], F32, name="tail%d_%d" % (d, half))
-            offsets = pos_t[d][:, half * HV // 16 : (half + 1) * HV // 16]
-            nc.vector.tensor_tensor(
-                tail[d, half][:], rows["h", last][:].indirect(offsets), gate[last][:, d, halves[half]], MULT
-            )
-
-        def first_add():
-            tail["part"] = keep.tile([P, V], F32, name="part")
-            nc.vector.tensor_tensor(tail["part"][:], msg[last, 0][:], msg[last, 1][:], ADD)
+        def first_add(half):
+            cols = halves[half]
+            nc.vector.tensor_tensor(part[:, cols], msg[last, 0][:, cols], msg[last, 1][:, cols], ADD)
 
         def second_add(half):
-            nc.vector.tensor_tensor(z[:, last, halves[half]], tail["part"][:, halves[half]], tail[2, half][:], ADD)
+            cols = halves[half]
+            nc.vector.tensor_tensor(z[:, last, cols], part[:, cols], msg[last, 2][:, cols], ADD)
 
         z_grouped = {}
 
@@ -356,10 +352,9 @@ def tile_picked_gatedg_none_po_kernel(
                 in_=z_grouped[half][:].rearrange("p v t -> p (v t)"),
             )
 
-        passed_on(last, 2)
-        passed_on_half(2, 0)
-        first_add()
-        passed_on_half(2, 1)
+        passed_on(last)
+        first_add(0)
+        first_add(1)
         second_add(0)
         group(0, nc.scalar.copy)
         second_add(1)

@@ -34,7 +34,7 @@ def tile_picked_gatedg_none_po_kernel(
         psum = ctx.enter_context(tc.psum_pool(name="psum", bufs=5))
         psum_sums = ctx.enter_context(tc.psum_pool(name="psum_sums", bufs=1))
 
-        reused = {"rows_e3": 0, "w3": 1024, "rows_h0": 2048, "rows_h1": 4096, "gates": 6144}
+        reused = {"rows_e3": 0, "w3": 1024, "rows_h0": 2048, "rows_h1": 4096, "pre2_2": 6144, "gates": 7168}
 
         def place(shape, label, tag=None):
             if label in reused:
@@ -294,8 +294,9 @@ def tile_picked_gatedg_none_po_kernel(
         cast_h(0, 1)
         cast_h(1, 1)
         empty("e", 3)
-        both_ends(2)
+        both_ends(2, 0, 2)
         quantise_h(2, 4)
+        both_ends(2, 2, 3)
         product("h", 2)
         product("h", 3)
         both_ends(3)

@@ -16,11 +16,15 @@ FP8X4 = mybir.dt.float8_e4m3fn_x4
 ADD = mybir.AluOpType.add
 MULT = mybir.AluOpType.mult
 SIGMOID = mybir.ActivationFunctionType.Sigmoid
+COPY = mybir.ActivationFunctionType.Copy
 
 P = 128
 PACK = 4
 HALF = N // 2
+L = P // 2
 EARLY = T // 2
+HV = V // 2
+TURNED = 2
 
 
 def tile_picked_gatedg_none_po_kernel(
@@ -31,10 +35,11 @@ def tile_picked_gatedg_none_po_kernel(
         lists = ctx.enter_context(tc.tile_pool(name="lists", bufs=1))
         keep = ctx.enter_context(tc.tile_pool(name="keep", bufs=1))
         late = ctx.enter_context(tc.tile_pool(name="late", bufs=1))
-        psum = ctx.enter_context(tc.psum_pool(name="psum", bufs=5))
-        psum_sums = ctx.enter_context(tc.psum_pool(name="psum_sums", bufs=1))
+        psum = ctx.enter_context(tc.psum_pool(name="psum", bufs=1))
 
-        reused = {"rows_e3": 0, "w3": 1024, "rows_h0": 2048, "rows_h1": 4096, "pre2_2": 6144, "gates": 7168}
+        reused = {
+            "w3": 0, "gate0": 7168, "pre1": 1024, "pre3": 4096, "gate_turned": 1024,
+        }
 
         def place(shape, label, tag=None):
             if label in reused:
@@ -47,10 +52,10 @@ def tile_picked_gatedg_none_po_kernel(
             return tile
 
         def load_half(name, w, half):
-            raw = place([P, PACK, HALF], name)
+            raw_half = place([P, PACK, HALF], name)
             cols = slice(half * HALF, (half + 1) * HALF)
-            nc.sync.dma_start(raw[:], w.rearrange("(p j) c -> p j c", j=PACK)[:, :, cols])
-            return raw
+            nc.sync.dma_start(raw_half[:], w.rearrange("(p j) c -> p j c", j=PACK)[:, :, cols])
+            return raw_half
 
         xs_all = keep.tile([P, T], U8, name="xs_all")
         nc.gpsimd.memset(xs_all[:].bitcast(I32), 0)
@@ -76,12 +81,11 @@ def tile_picked_gatedg_none_po_kernel(
         nc.scalar.activation(warm_out[:], warm_in[:], SIGMOID)
         load_words(slice(EARLY, T))
         raw["y", 0] = load_half("w1a", w1, 0)
+        cen_t = load_list("cen_t", cen)
         raw["e", 0] = load_half("w2a", w2, 0)
         raw["y", 1] = load_half("w1b", w1, 1)
-        cen_t = load_list("cen_t", cen)
-        pos_t = [load_list("pos0_t", pos1)]
         raw["e", 1] = load_half("w2b", w2, 1)
-        pos_t.extend([load_list("pos1_t", pos2), load_list("pos2_t", pos3)])
+        pos_t = [load_list("pos0_t", pos1), load_list("pos1_t", pos2), load_list("pos2_t", pos3)]
         raw_h = place([P, PACK, N], "w3")
         nc.sync.dma_start(raw_h[:], w3.rearrange("(p j) c -> p j c", j=PACK))
         for half in range(2):
@@ -93,235 +97,227 @@ def tile_picked_gatedg_none_po_kernel(
         xw = keep.tile([P, S], U32, name="xw", align_bytes=64)
         xs = keep.tile([P, S], U8, name="xs", align_bytes=64)
 
-        L = P // 2
-        grouped, codes, scales, rows = {}, {}, {}, {}
+        grouped, codes, scales = {}, {}, {}
+        for name in "yeh":
+            grouped[name] = keep.tile([P, PACK, 2, L, PACK], BF16, name="grouped_" + name, align_bytes=64)
+            codes[name] = keep.tile([P, N], U32, name="codes_" + name, align_bytes=64)
+            scales[name] = keep.tile([P, N], U8, name="scales_" + name, align_bytes=64)
 
-        def operand(name, block):
-            if (name, block) not in codes:
-                label = "%s%d" % (name, block)
-                codes[name, block] = keep.tile([P, P], U32, name="codes_" + label, align_bytes=64)
-                scales[name, block] = keep.tile([P, P], U8, name="scales_" + label, align_bytes=64)
-            return codes[name, block], scales[name, block]
-
-        def cast(name, half, first, last, copy):
-            if (name, half) not in grouped:
-                label = "grouped_%s%d" % (name, half)
-                grouped[name, half] = keep.tile([P, PACK, L, PACK], BF16, name=label, align_bytes=64)
+        def cast(name, half, pair, copy):
+            if pair == 0:
+                dst = grouped[name][:, half, :, :, :]
+            else:
+                dst = grouped[name][:, 2:4, half, :, :]
             copy(
-                grouped[name, half][:, first:last].rearrange("p t l j -> p l j t"),
-                raw[name, half][:].rearrange("p j (l t) -> p l j t", t=PACK)[:, :, :, first:last],
-            )
-
-        def quantise(name, half, pair):
-            if pair == 0:
-                words, plane = operand(name, half)
-                nc.vector.quantize_mx(
-                    out=words[:].bitcast(FP8X4),
-                    scales=plane[:],
-                    in_=grouped[name, half][:, 0:2].rearrange("p u l j -> p (u l j)"),
-                )
-            else:
-                cols = slice(half * L, (half + 1) * L)
-                for u in range(2):
-                    words, plane = operand(name, 2 + u)
-                    nc.vector.quantize_mx(
-                        out=words[:, cols].bitcast(FP8X4),
-                        scales=plane[:, cols],
-                        in_=grouped[name, half][:, 2 + u].rearrange("p l j -> p (l j)"),
-                    )
-
-        grouped_h = keep.tile([P, PACK, 2, L, PACK], BF16, name="grouped_h", align_bytes=64)
-        codes_h = keep.tile([P, N], U32, name="codes_h", align_bytes=64)
-        scales_h = keep.tile([P, N], U8, name="scales_h", align_bytes=64)
-
-        def cast_h(half, pair):
-            if pair == 0:
-                dst = grouped_h[:, half, :, :, :]
-            else:
-                dst = grouped_h[:, 2:4, half, :, :]
-            nc.scalar.copy(
                 dst.rearrange("p u l j -> p l j u"),
-                raw["h", half][:].rearrange("p j (l t) -> p l j t", t=PACK)[:, :, :, 2 * pair : 2 * pair + 2],
+                raw[name, half][:].rearrange("p j (l t) -> p l j t", t=PACK)[:, :, :, 2 * pair : 2 * pair + 2],
             )
 
-        def quantise_h(first, last):
+        def quantise(name, first, last):
             cols = slice(first * P, last * P)
             nc.vector.quantize_mx(
-                out=codes_h[:, cols].bitcast(FP8X4),
-                scales=scales_h[:, cols],
-                in_=grouped_h[:, first:last].rearrange("p a b l j -> p (a b l j)"),
+                out=codes[name][:, cols].bitcast(FP8X4),
+                scales=scales[name][:, cols],
+                in_=grouped[name][:, first:last].rearrange("p a b l j -> p (a b l j)"),
             )
-            for block in range(first, last):
-                codes["h", block] = codes_h[:, block * P : (block + 1) * P]
-                scales["h", block] = scales_h[:, block * P : (block + 1) * P]
 
-        banks = {}
+        banks, rows = {}, {}
 
-        def product(name, t):
-            bank = psum.tile([P, S], F32, name="bank")
+        def product(name, t, tag):
+            cols = slice(t * P, (t + 1) * P)
+            banks[name, t] = psum.tile([P, S], F32, name="bank_%s%d" % (name, t), tag=tag)
             nc.tensor.matmul_mx(
-                out=bank[:],
-                lhsT=codes[name, t][:].bitcast(FP8X4),
-                lhsT_scale=scales[name, t][:],
+                out=banks[name, t][:],
+                lhsT=codes[name][:, cols].bitcast(FP8X4),
+                lhsT_scale=scales[name][:, cols],
                 rhs=xw[:].bitcast(FP8X4),
                 rhs_scale=xs[:],
                 start=True,
                 stop=True,
             )
-            banks[name, t] = bank
 
         def empty(name, t, tag=None):
-            label = "rows_%s%d" % (name, t)
-            if name == "y" and t > 0:
-                if t == 1:
-                    rows["y", "rest"] = keep.tile([P, 3, S], F32, name="rows_y_rest", tag="w2b", align_bytes=64)
-                rows[name, t] = rows["y", "rest"][:, t - 1, :]
-            else:
-                rows[name, t] = place([P, S], label, tag)
+            rows[name, t] = place([P, S], "rows_%s%d" % (name, t), tag)
             nc.scalar.copy(rows[name, t][:], banks[name, t][:])
 
-        yc, pre, gate = {}, {}, {}
+        yc, pre, gate, msg, turned = {}, {}, {}, {}, {}
 
-        def centre(t, tag=None):
-            if t == 0:
-                yc["all"] = keep.tile([P, PACK, V], F32, name="centres", align_bytes=64)
-            yc[t] = yc["all"][:, t, :]
-            nc.vector.tensor_copy(yc[t][:], rows["y", t][:].indirect(cen_t[:]))
+        def centre(t):
+            yc[t] = place([P, V], "yc%d" % t)
+            nc.scalar.activation(yc[t][:], rows["y", t][:].indirect(cen_t[:]), COPY)
 
-        def both_ends(t, first=0, last=3, tag=None):
-            label = "pre%d_%d" % (t, first)
-            part = place([P, last - first, V], label, tag)
+        def both_ends(t, first=0, last=3, label=None):
+            part = place([P, last - first, V], label or "pre%d" % t)
             pre.setdefault(t, []).append((first, last, part))
             for d in range(first, last):
                 nc.vector.tensor_tensor(part[:, d - first, :], rows["e", t][:].indirect(pos_t[d][:]), yc[t][:], ADD)
 
         def squash(t):
-            if t == 0:
-                gate["all"] = place([P, PACK, 3, V], "gates")
-            gate[t] = gate["all"][:, t]
+            gate[t] = place([P, 3, V], "gate%d" % t)
             for first, last, part in pre[t]:
                 nc.scalar.activation(gate[t][:, first:last, :], part[:], SIGMOID)
 
-        z = keep.tile([P, PACK, V], F32, name="z")
-        out_rows = out_0.rearrange("(p t) v -> p t v", t=PACK)
-        msg, turned = {}, {}
-        held01 = keep.tile([P, 2, 2, P], F32, name="held01")
-        held2 = keep.tile([P, 2, P], F32, name="held2")
-
-        def passed_on(t):
-            for d in range(3):
-                msg[t, d] = keep.tile([P, V], F32, name="msg%d_%d" % (t, d))
+        def passed_on(t, first=0, last=3):
+            for d in range(first, last):
+                msg[t, d] = place([P, V], "msg%d_%d" % (t, d))
                 nc.vector.tensor_tensor(msg[t, d][:], rows["h", t][:].indirect(pos_t[d][:]), gate[t][:, d, :], MULT)
 
+        z = keep.tile([P, PACK, V], F32, name="z")
+        out_rows = out_0.rearrange("(p t) v -> p t v", t=PACK)
+        held = {}
+
         def turn(t):
+            turned[t] = psum.tile([P, 2, P], F32, name="turned%d" % t, tag="EB"[t])
             for half in range(2):
-                turned[t, half] = psum_sums.tile([P, P], F32, name="turned%d" % half)
-            for d in range(3):
-                for half in range(2):
+                for d in range(3):
                     nc.tensor.matmul(
-                        turned[t, half][:], msg[t, d][:, half * P : (half + 1) * P], identity[:],
+                        turned[t][:, half, :], msg[t, d][:, half * P : (half + 1) * P], identity[:],
                         start=d == 0, stop=d == 2, is_transpose=True,
                     )
 
         def hold(t):
+            if t == 0:
+                held["sums"] = place([P, 2, 2, P], "held01", "rows_h2")
+            nc.scalar.copy(
+                held["sums"][:, :, :, t * L : (t + 1) * L], turned[t][:].rearrange("v h (u l) -> v h u l", u=2)
+            )
+
+        picked, sides = {}, {}
+
+        def pick(name, d, on_scalar_engine=True):
+            picked[name, d] = place([P, V], "picked_%s%d" % (name, d))
+            window = rows[name, TURNED][:].indirect(pos_t[d][:])
+            if on_scalar_engine:
+                nc.scalar.activation(picked[name, d][:], window, COPY)
+            else:
+                nc.vector.tensor_copy(picked[name, d][:], window)
+
+        def turn_both_ends():
+            for half, tag in enumerate("DA"):
+                cols = slice(half * P, (half + 1) * P)
+                sides["pre", half] = psum.tile([P, 3, P], F32, name="pre_turned%d" % half, tag=tag)
+                for d in range(3):
+                    for src, first in ((yc[TURNED], True), (picked["e", d], False)):
+                        nc.tensor.matmul(
+                            sides["pre", half][:, d, :], src[:, cols], identity[:],
+                            start=first, stop=not first, is_transpose=True,
+                        )
+
+        def squash_turned():
+            gate[TURNED] = place([P, 2, 3, P], "gate_turned")
             for half in range(2):
-                if t < 2:
-                    nc.scalar.copy(
-                        held01[:, half, :, t * L : (t + 1) * L], turned[t, half][:].rearrange("v (u l) -> v u l", u=2)
+                nc.scalar.activation(gate[TURNED][:, half], sides["pre", half][:], SIGMOID)
+
+        def turn_passed_on():
+            for half, tag in enumerate("GF"):
+                sides["h", half] = psum.tile([P, 3, P], F32, name="h_turned%d" % half, tag=tag)
+            for d in range(3):
+                for half in range(2):
+                    nc.tensor.transpose(
+                        sides["h", half][:, d, :], picked["h", d][:, half * P : (half + 1) * P], identity[:]
                     )
-                else:
-                    nc.scalar.copy(held2[:, half, :], turned[t, half][:])
+
+        def weigh_turned(half):
+            msg[TURNED, half] = place([P, 3, P], "msg_turned%d" % half)
+            nc.vector.tensor_tensor(msg[TURNED, half][:], sides["h", half][:], gate[TURNED][:, half], MULT)
 
         def back01():
-            back = psum_sums.tile([P, 2, 2, P], F32, name="back")
+            back = psum.tile([P, 2, 2, P], F32, name="back01", tag="H")
             for u in range(2):
                 for half in range(2):
-                    nc.tensor.transpose(back[:, u, half, :], held01[:, half, u, :], identity[:])
+                    nc.tensor.transpose(back[:, u, half, :], held["sums"][:, half, u, :], identity[:])
             nc.scalar.copy(z[:, 0:2, :], back[:].rearrange("p u h v -> p u (h v)"))
             nc.sync.dma_start(out_rows[:, 0:2, :], z[:, 0:2, :])
 
-        def back2():
+        def back_turned():
+            back = psum.tile([P, 2, P], F32, name="back_turned", tag="D")
             for half in range(2):
-                back = psum.tile([P, P], F32, name="bank")
-                nc.tensor.transpose(back[:], held2[:, half, :], identity[:])
-                nc.scalar.copy(z[:, 2, half * P : (half + 1) * P], back[:])
-            nc.sync.dma_start(out_rows[:, 2, :], z[:, 2, :])
+                for d in range(3):
+                    nc.tensor.matmul(
+                        back[:, half, :], msg[TURNED, half][:, d, :], identity[:],
+                        start=d == 0, stop=d == 2, is_transpose=True,
+                    )
+            nc.scalar.copy(z[:, TURNED, :], back[:].rearrange("p h v -> p (h v)"))
+            nc.sync.dma_start(out_rows[:, TURNED, :], z[:, TURNED, :])
 
         on_scalar, on_vector = nc.scalar.copy, nc.vector.tensor_copy
         nc.vector.tensor_copy(xs[:], xs_all[:].indirect(offs_t[:]))
         nc.vector.tensor_copy(xw[:], xw_all[:].indirect(offs_t[:]))
-        cast("y", 0, 0, 2, on_scalar)
-        quantise("y", 0, 0)
-        product("y", 0)
-        cast("y", 0, 2, 4, on_scalar)
+        cast("y", 0, 0, on_scalar)
         quantise("y", 0, 1)
-        cast("e", 0, 0, 2, on_vector)
-        cast("e", 0, 2, 4, on_scalar)
-        quantise("e", 0, 0)
-        product("e", 0)
+        product("y", 0, "A")
+        cast("y", 0, 1, on_scalar)
+        cast("e", 0, 0, on_vector)
+        cast("e", 0, 1, on_vector)
         quantise("e", 0, 1)
-        empty("y", 0, "w2a")
-        empty("e", 0)
-        cast("y", 1, 0, 4, on_vector)
+        product("e", 0, "B")
+        empty("y", 0)
         centre(0)
-        quantise("y", 1, 0)
-        product("y", 1)
-        quantise("y", 1, 1)
-        product("y", 2)
-        product("y", 3)
-        cast("e", 1, 0, 2, on_scalar)
-        cast("e", 1, 2, 4, on_scalar)
+        empty("e", 0)
+        cast("y", 1, 0, on_vector)
+        cast("y", 1, 1, on_vector)
+        quantise("y", 1, 2)
+        product("y", 1, "C")
+        quantise("y", 2, 4)
+        product("y", 3, "E")
+        product("y", 2, "D")
+        cast("e", 1, 0, on_vector)
+        cast("e", 1, 1, on_vector)
+        quantise("e", 1, 2)
+        product("e", 1, "A")
+        quantise("e", 2, 4)
+        product("e", 3, "B")
         both_ends(0)
-        quantise("e", 1, 0)
-        product("e", 1)
-        quantise("e", 1, 1)
-        product("e", 2)
-        product("e", 3)
         empty("y", 1)
-        empty("y", 2)
+        product("e", 2, "C")
         empty("y", 3)
-        empty("e", 1)
         centre(1)
-        centre(2)
+        empty("y", 2)
         centre(3)
-        both_ends(1)
-        cast_h(0, 0)
+        empty("e", 1)
+        centre(2)
         empty("e", 2)
-        cast_h(1, 0)
-        quantise_h(0, 2)
-        product("h", 0)
-        product("h", 1)
-        cast_h(0, 1)
-        cast_h(1, 1)
         empty("e", 3)
-        both_ends(2, 0, 2)
-        quantise_h(2, 4)
-        both_ends(2, 2, 3)
-        product("h", 2)
-        product("h", 3)
+        pick("e", 0)
+        pick("e", 1)
+        pick("e", 2)
+        cast("h", 0, 0, on_vector)
+        cast("h", 1, 0, on_vector)
+        cast("h", 0, 1, on_vector)
+        cast("h", 1, 1, on_vector)
+        quantise("h", 0, 2)
+        product("h", 0, "D")
+        product("h", 1, "A")
+        quantise("h", 2, 4)
+        product("h", 2, "C")
+        product("h", 3, "B")
+        both_ends(1)
         both_ends(3)
-        squash(0)
         empty("h", 0)
-        squash(1)
+        squash(0)
         passed_on(0)
         empty("h", 1)
-        squash(2)
+        turn_both_ends()
+        squash(1)
         passed_on(1)
         empty("h", 2)
-        passed_on(2)
+        squash_turned()
+        pick("h", 0)
+        pick("h", 1)
+        pick("h", 2, False)
+        turn_passed_on()
+        weigh_turned(0)
+        weigh_turned(1)
+        empty("h", 3)
         squash(3)
         turn(0)
         hold(0)
-        empty("h", 3)
         turn(1)
         hold(1)
+        back_turned()
         back01()
-        turn(2)
-        hold(2)
-        back2()
 
         last = PACK - 1
-        HV = V // 2
         halves = [slice(0, HV), slice(HV, V)]
         part = keep.tile([P, V], F32, name="part")
 

@@ -38,7 +38,8 @@ def tile_picked_gatedg_none_po_kernel(
         psum = ctx.enter_context(tc.psum_pool(name="psum", bufs=1))
 
         reused = {
-            "w3": 0, "gate0": 7168, "pre1": 1024, "pre3": 4096, "gate_turned": 1024,
+            "w3": 0, "picked_e0": 0, "gate0": 7168,
+            "w2b": 12288, "yc1": 12288, "yc3": 13312, "pre0": 14336,"pre1": 1024, "pre3": 4096, "gate_turned": 1024,
         }
 
         def place(shape, label, tag=None):
@@ -81,15 +82,13 @@ def tile_picked_gatedg_none_po_kernel(
         nc.scalar.activation(warm_out[:], warm_in[:], SIGMOID)
         load_words(slice(EARLY, T))
         raw["y", 0] = load_half("w1a", w1, 0)
-        cen_t = load_list("cen_t", cen)
-        raw["e", 0] = load_half("w2a", w2, 0)
         raw["y", 1] = load_half("w1b", w1, 1)
+        raw["e", 0] = load_half("w2a", w2, 0)
+        cen_t = load_list("cen_t", cen)
         raw["e", 1] = load_half("w2b", w2, 1)
         pos_t = [load_list("pos0_t", pos1), load_list("pos1_t", pos2), load_list("pos2_t", pos3)]
         raw_h = place([P, PACK, N], "w3")
         nc.sync.dma_start(raw_h[:], w3.rearrange("(p j) c -> p j c", j=PACK))
-        for half in range(2):
-            raw["h", half] = raw_h[:, :, half * HALF : (half + 1) * HALF]
 
         identity = keep.tile([P, P], F32, name="identity")
         make_identity(nc, identity[:])
@@ -112,6 +111,14 @@ def tile_picked_gatedg_none_po_kernel(
                 dst.rearrange("p u l j -> p l j u"),
                 raw[name, half][:].rearrange("p j (l t) -> p l j t", t=PACK)[:, :, :, 2 * pair : 2 * pair + 2],
             )
+
+        def cast_whole(pair):
+            if pair == 0:
+                dst = grouped["h"][:, 0:2].rearrange("p half u l j -> p half l j u")
+            else:
+                dst = grouped["h"][:, 2:4].rearrange("p u half l j -> p half l j u")
+            src = raw_h[:].rearrange("p j (half l t) -> p half l j t", half=2, t=PACK)
+            nc.vector.tensor_copy(dst, src[:, :, :, :, 2 * pair : 2 * pair + 2])
 
         def quantise(name, first, last):
             cols = slice(first * P, last * P)
@@ -142,9 +149,15 @@ def tile_picked_gatedg_none_po_kernel(
 
         yc, pre, gate, msg, turned = {}, {}, {}, {}, {}
 
-        def centre(t):
+        def fetch(dst, window, on_scalar_engine):
+            if on_scalar_engine:
+                nc.scalar.activation(dst, window, COPY)
+            else:
+                nc.vector.tensor_copy(dst, window)
+
+        def centre(t, on_scalar_engine=True):
             yc[t] = place([P, V], "yc%d" % t)
-            nc.scalar.activation(yc[t][:], rows["y", t][:].indirect(cen_t[:]), COPY)
+            fetch(yc[t][:], rows["y", t][:].indirect(cen_t[:]), on_scalar_engine)
 
         def both_ends(t, first=0, last=3, label=None):
             part = place([P, last - first, V], label or "pre%d" % t)
@@ -186,11 +199,7 @@ def tile_picked_gatedg_none_po_kernel(
 
         def pick(name, d, on_scalar_engine=True):
             picked[name, d] = place([P, V], "picked_%s%d" % (name, d))
-            window = rows[name, TURNED][:].indirect(pos_t[d][:])
-            if on_scalar_engine:
-                nc.scalar.activation(picked[name, d][:], window, COPY)
-            else:
-                nc.vector.tensor_copy(picked[name, d][:], window)
+            fetch(picked[name, d][:], rows[name, TURNED][:].indirect(pos_t[d][:]), on_scalar_engine)
 
         def turn_both_ends():
             for half, tag in enumerate("DA"):
@@ -247,30 +256,30 @@ def tile_picked_gatedg_none_po_kernel(
         quantise("y", 0, 1)
         product("y", 0, "A")
         cast("y", 0, 1, on_scalar)
-        cast("e", 0, 0, on_vector)
-        cast("e", 0, 1, on_vector)
-        quantise("e", 0, 1)
-        product("e", 0, "B")
-        empty("y", 0)
-        centre(0)
-        empty("e", 0)
         cast("y", 1, 0, on_vector)
-        cast("y", 1, 1, on_vector)
+        cast("y", 1, 1, on_scalar)
+        empty("y", 0)
         quantise("y", 1, 2)
         product("y", 1, "C")
         quantise("y", 2, 4)
         product("y", 3, "E")
-        product("y", 2, "D")
+        cast("e", 0, 0, on_vector)
+        cast("e", 0, 1, on_vector)
+        quantise("e", 0, 1)
+        product("e", 0, "B")
+        centre(0, False)
+        empty("y", 1)
         cast("e", 1, 0, on_vector)
         cast("e", 1, 1, on_vector)
         quantise("e", 1, 2)
         product("e", 1, "A")
         quantise("e", 2, 4)
-        product("e", 3, "B")
-        both_ends(0)
-        empty("y", 1)
         product("e", 2, "C")
+        product("e", 3, "D")
         empty("y", 3)
+        empty("e", 0)
+        product("y", 2, "B")
+        both_ends(0)
         centre(1)
         empty("y", 2)
         centre(3)
@@ -278,13 +287,10 @@ def tile_picked_gatedg_none_po_kernel(
         centre(2)
         empty("e", 2)
         empty("e", 3)
-        pick("e", 0)
         pick("e", 1)
         pick("e", 2)
-        cast("h", 0, 0, on_vector)
-        cast("h", 1, 0, on_vector)
-        cast("h", 0, 1, on_vector)
-        cast("h", 1, 1, on_vector)
+        cast_whole(0)
+        cast_whole(1)
         quantise("h", 0, 2)
         product("h", 0, "D")
         product("h", 1, "A")
@@ -292,19 +298,20 @@ def tile_picked_gatedg_none_po_kernel(
         product("h", 2, "C")
         product("h", 3, "B")
         both_ends(1)
+        pick("e", 0, False)
         both_ends(3)
         empty("h", 0)
         squash(0)
         passed_on(0)
         empty("h", 1)
         turn_both_ends()
+        empty("h", 2)
+        pick("h", 2, False)
         squash(1)
         passed_on(1)
-        empty("h", 2)
         squash_turned()
         pick("h", 0)
         pick("h", 1)
-        pick("h", 2, False)
         turn_passed_on()
         weigh_turned(0)
         weigh_turned(1)

@@ -38,8 +38,8 @@ def tile_picked_gatedg_none_po_kernel(
         psum = ctx.enter_context(tc.psum_pool(name="psum", bufs=1))
 
         reused = {
-            "w3": 0, "picked_e0": 0, "gate0": 7168,
-            "w2b": 12288, "yc1": 12288, "yc3": 13312, "pre0": 14336,"pre1": 1024, "pre3": 4096, "gate_turned": 1024,
+            "w3": 0, "gate0": 7168,
+            "w2b": 12288, "rows_y2": 11264, "yc1": 13312, "yc3": 14336, "pre0": 15360,"pre1": 1024, "pre3": 4096, "gate_turned": 1024,
         }
 
         def place(shape, label, tag=None):
@@ -277,8 +277,8 @@ def tile_picked_gatedg_none_po_kernel(
         product("e", 2, "C")
         product("e", 3, "D")
         empty("y", 3)
+        product("y", 2, "E")
         empty("e", 0)
-        product("y", 2, "B")
         both_ends(0)
         centre(1)
         empty("y", 2)
@@ -287,6 +287,7 @@ def tile_picked_gatedg_none_po_kernel(
         centre(2)
         empty("e", 2)
         empty("e", 3)
+        pick("e", 0)
         pick("e", 1)
         pick("e", 2)
         cast_whole(0)
@@ -298,7 +299,6 @@ def tile_picked_gatedg_none_po_kernel(
         product("h", 2, "C")
         product("h", 3, "B")
         both_ends(1)
-        pick("e", 0, False)
         both_ends(3)
         empty("h", 0)
         squash(0)
@@ -317,6 +317,8 @@ def tile_picked_gatedg_none_po_kernel(
         weigh_turned(1)
         empty("h", 3)
         squash(3)
+        picked_last = place([P, V], "picked_last")
+        fetch(picked_last[:], rows["h", 3][:].indirect(pos_t[0][:]), True)
         turn(0)
         hold(0)
         turn(1)
@@ -330,11 +332,11 @@ def tile_picked_gatedg_none_po_kernel(
 
         def first_add(half):
             cols = halves[half]
-            nc.vector.tensor_tensor(part[:, cols], msg[last, 0][:, cols], msg[last, 1][:, cols], ADD)
+            nc.vector.tensor_tensor(part[:, cols], msg[last, 1][:, cols], msg[last, 2][:, cols], ADD)
 
         def second_add(half):
             cols = halves[half]
-            nc.vector.tensor_tensor(z[:, last, cols], part[:, cols], msg[last, 2][:, cols], ADD)
+            nc.vector.tensor_tensor(z[:, last, cols], part[:, cols], msg[last, 0][:, cols], ADD)
 
         z_grouped = {}
 
@@ -356,7 +358,9 @@ def tile_picked_gatedg_none_po_kernel(
                 in_=z_grouped[half][:].rearrange("p v t -> p (v t)"),
             )
 
-        passed_on(last)
+        passed_on(last, 1, 3)
+        msg[last, 0] = place([P, V], "msg_last")
+        nc.vector.tensor_tensor(msg[last, 0][:], picked_last[:], gate[last][:, 0, :], MULT)
         first_add(0)
         first_add(1)
         second_add(0)

@@ -38,6 +38,7 @@ def tile_picked_gatedg_none_po_kernel(
         psum = ctx.enter_context(tc.psum_pool(name="psum", bufs=1))
 
         reused = {
+            "yc2": 20480,
             "w3": 0, "gate0": 7168,
             "w2b": 12288, "rows_y2": 11264, "yc1": 13312, "yc3": 14336, "pre0": 15360,"pre1": 1024, "pre3": 4096, "gate_turned": 1024,
         }
@@ -89,6 +90,8 @@ def tile_picked_gatedg_none_po_kernel(
         pos_t = [load_list("pos0_t", pos1), load_list("pos1_t", pos2), load_list("pos2_t", pos3)]
         raw_h = place([P, PACK, N], "w3")
         nc.sync.dma_start(raw_h[:], w3.rearrange("(p j) c -> p j c", j=PACK))
+        for half in range(2):
+            raw["h", half] = raw_h[:, :, half * HALF : (half + 1) * HALF]
 
         identity = keep.tile([P, P], F32, name="identity")
         make_identity(nc, identity[:])
@@ -98,34 +101,25 @@ def tile_picked_gatedg_none_po_kernel(
 
         grouped, codes, scales = {}, {}, {}
         for name in "yeh":
-            grouped[name] = keep.tile([P, PACK, 2, L, PACK], BF16, name="grouped_" + name, align_bytes=64)
+            if name == "h":
+                grouped[name] = late.tile([P, 2 * PACK, L, PACK], BF16, name="grouped_h", offset=reused["yc2"], align_bytes=64)
+            else:
+                grouped[name] = keep.tile([P, 2 * PACK, L, PACK], BF16, name="grouped_" + name, align_bytes=64)
             codes[name] = keep.tile([P, N], U32, name="codes_" + name, align_bytes=64)
             scales[name] = keep.tile([P, N], U8, name="scales_" + name, align_bytes=64)
 
-        def cast(name, half, pair, copy):
-            if pair == 0:
-                dst = grouped[name][:, half, :, :, :]
-            else:
-                dst = grouped[name][:, 2:4, half, :, :]
+        def cast(name, half, first, last, runs, copy):
             copy(
-                dst.rearrange("p u l j -> p l j u"),
-                raw[name, half][:].rearrange("p j (l t) -> p l j t", t=PACK)[:, :, :, 2 * pair : 2 * pair + 2],
+                grouped[name][:, runs].rearrange("p t l j -> p l j t"),
+                raw[name, half][:].rearrange("p j (l t) -> p l j t", t=PACK)[:, :, :, first:last],
             )
 
-        def cast_whole(pair):
-            if pair == 0:
-                dst = grouped["h"][:, 0:2].rearrange("p half u l j -> p half l j u")
-            else:
-                dst = grouped["h"][:, 2:4].rearrange("p u half l j -> p half l j u")
-            src = raw_h[:].rearrange("p j (half l t) -> p half l j t", half=2, t=PACK)
-            nc.vector.tensor_copy(dst, src[:, :, :, :, 2 * pair : 2 * pair + 2])
-
-        def quantise(name, first, last):
-            cols = slice(first * P, last * P)
+        def quantise(name, first, last, to):
+            cols = slice(to * L, (to + last - first) * L)
             nc.vector.quantize_mx(
                 out=codes[name][:, cols].bitcast(FP8X4),
                 scales=scales[name][:, cols],
-                in_=grouped[name][:, first:last].rearrange("p a b l j -> p (a b l j)"),
+                in_=grouped[name][:, first:last].rearrange("p r l j -> p (r l j)"),
             )
 
         banks, rows = {}, {}
@@ -202,7 +196,7 @@ def tile_picked_gatedg_none_po_kernel(
             fetch(picked[name, d][:], rows[name, TURNED][:].indirect(pos_t[d][:]), on_scalar_engine)
 
         def turn_both_ends():
-            for half, tag in enumerate("DA"):
+            for half, tag in enumerate("HF"):
                 cols = slice(half * P, (half + 1) * P)
                 sides["pre", half] = psum.tile([P, 3, P], F32, name="pre_turned%d" % half, tag=tag)
                 for d in range(3):
@@ -228,7 +222,12 @@ def tile_picked_gatedg_none_po_kernel(
 
         def weigh_turned(half):
             msg[TURNED, half] = place([P, 3, P], "msg_turned%d" % half)
-            nc.vector.tensor_tensor(msg[TURNED, half][:], sides["h", half][:], gate[TURNED][:, half], MULT)
+            nc.vector.tensor_tensor(
+                msg[TURNED, half][:].rearrange("v d (r l) -> v d r l", r=2),
+                sides["h", half][:].rearrange("v d (r l) -> v d r l", r=2)[:, :, ::-1, :],
+                gate[TURNED][:, half].rearrange("v d (r l) -> v d r l", r=2)[:, :, ::-1, :],
+                MULT,
+            )
 
         def back01():
             back = psum.tile([P, 2, 2, P], F32, name="back01", tag="H")
@@ -252,28 +251,29 @@ def tile_picked_gatedg_none_po_kernel(
         on_scalar, on_vector = nc.scalar.copy, nc.vector.tensor_copy
         nc.vector.tensor_copy(xs[:], xs_all[:].indirect(offs_t[:]))
         nc.vector.tensor_copy(xw[:], xw_all[:].indirect(offs_t[:]))
-        cast("y", 0, 0, on_scalar)
-        quantise("y", 0, 1)
+        cast("y", 0, 0, 2, slice(0, 2), on_scalar)
+        quantise("y", 0, 2, 0)
         product("y", 0, "A")
-        cast("y", 0, 1, on_scalar)
-        cast("y", 1, 0, on_vector)
-        cast("y", 1, 1, on_scalar)
+        cast("y", 0, 2, 4, slice(5, 7), on_scalar)
+        cast("y", 1, 0, 2, slice(2, 4), on_vector)
+        cast("y", 1, 2, 4, slice(4, 8, 3), on_scalar)
         empty("y", 0)
-        quantise("y", 1, 2)
+        quantise("y", 2, 4, 2)
         product("y", 1, "C")
-        quantise("y", 2, 4)
+        quantise("y", 4, 8, 4)
         product("y", 3, "E")
-        cast("e", 0, 0, on_vector)
-        cast("e", 0, 1, on_vector)
-        quantise("e", 0, 1)
+        cast("e", 0, 0, 2, slice(0, 2), on_vector)
+        cast("e", 0, 2, 4, slice(2, 4), on_vector)
+        quantise("e", 0, 2, 0)
         product("e", 0, "B")
+        quantise("e", 2, 4, 5)
         centre(0, False)
         empty("y", 1)
-        cast("e", 1, 0, on_vector)
-        cast("e", 1, 1, on_vector)
-        quantise("e", 1, 2)
+        cast("e", 1, 0, 4, slice(4, 8), on_vector)
+        quantise("e", 4, 6, 2)
         product("e", 1, "A")
-        quantise("e", 2, 4)
+        quantise("e", 6, 7, 4)
+        quantise("e", 7, 8, 7)
         product("e", 2, "C")
         product("e", 3, "D")
         empty("y", 3)
@@ -284,27 +284,30 @@ def tile_picked_gatedg_none_po_kernel(
         empty("y", 2)
         centre(3)
         empty("e", 1)
-        centre(2)
         empty("e", 2)
         empty("e", 3)
         pick("e", 0)
         pick("e", 1)
         pick("e", 2)
-        cast_whole(0)
-        cast_whole(1)
-        quantise("h", 0, 2)
+        cast("h", 0, 0, 4, slice(0, 4), on_vector)
+        cast("h", 1, 0, 4, slice(4, 8), on_vector)
+        quantise("h", 0, 2, 0)
         product("h", 0, "D")
+        quantise("h", 2, 4, 5)
+        quantise("h", 4, 6, 2)
         product("h", 1, "A")
-        quantise("h", 2, 4)
+        quantise("h", 6, 7, 4)
+        quantise("h", 7, 8, 7)
         product("h", 2, "C")
         product("h", 3, "B")
         both_ends(1)
         both_ends(3)
-        empty("h", 0)
         squash(0)
+        empty("h", 0)
+        centre(2)
+        turn_both_ends()
         passed_on(0)
         empty("h", 1)
-        turn_both_ends()
         empty("h", 2)
         pick("h", 2, False)
         squash(1)
@@ -338,13 +341,12 @@ def tile_picked_gatedg_none_po_kernel(
             cols = halves[half]
             nc.vector.tensor_tensor(z[:, last, cols], part[:, cols], msg[last, 0][:, cols], ADD)
 
-        z_grouped = {}
+        z_grouped = keep.tile([P, V, PACK], BF16, name="z_grouped", align_bytes=64)
 
-        def group(half, copy):
-            z_grouped[half] = keep.tile([P, HV, PACK], BF16, name="z_grouped%d" % half, align_bytes=64)
+        def group(cols, copy):
             copy(
-                z_grouped[half][:].rearrange("p (c i) t -> p c t i", i=4),
-                z[:, :, halves[half]].rearrange("p t (c i) -> p c t i", i=4),
+                z_grouped[:, cols].rearrange("p (c i) t -> p c t i", i=4),
+                z[:, :, cols].rearrange("p t (c i) -> p c t i", i=4),
             )
 
         z_codes = keep.tile([P, V], U32, name="z_codes", align_bytes=64)
@@ -355,21 +357,22 @@ def tile_picked_gatedg_none_po_kernel(
             nc.vector.quantize_mx(
                 out=z_codes[:, halves[half]].bitcast(FP8X4),
                 scales=z_scales[:, halves[half]],
-                in_=z_grouped[half][:].rearrange("p v t -> p (v t)"),
+                in_=z_grouped[:, halves[half]].rearrange("p v t -> p (v t)"),
             )
 
         passed_on(last, 1, 3)
         msg[last, 0] = place([P, V], "msg_last")
         nc.vector.tensor_tensor(msg[last, 0][:], picked_last[:], gate[last][:, 0, :], MULT)
-        first_add(0)
         first_add(1)
-        second_add(0)
-        group(0, nc.scalar.copy)
+        first_add(0)
         second_add(1)
+        second_add(0)
         nc.sync.dma_start(out_rows[:, last, :], z[:, last, :])
-        group(1, nc.vector.tensor_copy)
-        hand_on(0)
+        group(halves[1], nc.vector.tensor_copy)
+        group(slice(0, HV // 2), nc.scalar.copy)
+        group(slice(HV // 2, HV), nc.vector.tensor_copy)
         hand_on(1)
+        hand_on(0)
         nc.sync.dma_start(words_out, z_codes[:].bitcast(I32))
         for q in range(4):
             queue = nc.sync if q % 2 == 1 else nc.scalar

@@ -60,7 +60,7 @@ def tile_picked_gatedg_none_po_kernel(
             return raw_half
 
         xs_all = keep.tile([P, T], U8, name="xs_all")
-        nc.gpsimd.memset(xs_all[:].bitcast(I32), 0)
+        nc.vector.memset(xs_all[:].bitcast(I32), 0)
         xw_all = keep.tile([P, T], U32, name="xw_all")
 
         def load_words(cols):
@@ -76,7 +76,7 @@ def tile_picked_gatedg_none_po_kernel(
         raw = {}
         warm_in = keep.tile([P, 1], F32, name="warm_in")
         warm_out = keep.tile([P, 1], F32, name="warm_out")
-        nc.gpsimd.memset(warm_in[:], 0.0)
+        nc.vector.memset(warm_in[:], 0.0)
         load_words(slice(0, EARLY))
         offs_t = load_list("offs_t", offs)
         load_scales((nc.scalar, nc.scalar, nc.sync, nc.sync))

@@ -74,7 +74,7 @@ def tile_picked_gatedg_none_po_kernel(
                 )
 
         raw = {}
-        warm_in = keep.tile([P, 1], F32, name="warm_in")
+        warm_in = keep.tile([P, 1], F32, name="warm_in", tag="identity")
         warm_out = keep.tile([P, 1], F32, name="warm_out")
         nc.vector.memset(warm_in[:], 0.0)
         load_words(slice(0, EARLY))
@@ -93,7 +93,7 @@ def tile_picked_gatedg_none_po_kernel(
         for half in range(2):
             raw["h", half] = raw_h[:, :, half * HALF : (half + 1) * HALF]
 
-        identity = keep.tile([P, P], F32, name="identity")
+        identity = keep.tile([P, P], F32, name="identity", tag="identity")
         make_identity(nc, identity[:])
 
         xw = keep.tile([P, S], U32, name="xw", align_bytes=64)

@@ -22,7 +22,7 @@ P = 128
 PACK = 4
 HALF = N // 2
 L = P // 2
-EARLY = T // 2
+EARLY = 5 * T // 8
 HV = V // 2
 TURNED = 2
 

@@ -345,8 +345,8 @@ def tile_picked_gatedg_none_po_kernel(
 
         def group(cols, copy):
             copy(
-                z_grouped[:, cols].rearrange("p (c i) t -> p c t i", i=4),
-                z[:, :, cols].rearrange("p t (c i) -> p c t i", i=4),
+                z_grouped[:, cols].rearrange("p (c i) t -> p c t i", i=2),
+                z[:, :, cols].rearrange("p t (c i) -> p c t i", i=2),
             )
 
         z_codes = keep.tile([P, V], U32, name="z_codes", align_bytes=64)

@@ -269,7 +269,8 @@ def tile_picked_gatedg_none_po_kernel(
         quantise("e", 2, 4, 5)
         centre(0, False)
         empty("y", 1)
-        cast("e", 1, 0, 4, slice(4, 8), on_vector)
+        cast("e", 1, 0, 2, slice(4, 6), on_vector)
+        cast("e", 1, 2, 4, slice(6, 8), on_vector)
         quantise("e", 4, 6, 2)
         product("e", 1, "A")
         quantise("e", 6, 7, 4)

from contextlib import ExitStack

import concourse.mybir as mybir
from concourse.masks import make_identity

K, T, S, V, N = 512, 1024, 512, 256, 512
FLOPS = 3 * 2 * K * N * S

F32 = mybir.dt.float32
BF16 = mybir.dt.bfloat16
I32 = mybir.dt.int32
U32 = mybir.dt.uint32
U16 = mybir.dt.uint16
U8 = mybir.dt.uint8
FP8X4 = mybir.dt.float8_e4m3fn_x4
ADD = mybir.AluOpType.add
MULT = mybir.AluOpType.mult
SIGMOID = mybir.ActivationFunctionType.Sigmoid
COPY = mybir.ActivationFunctionType.Copy

P = 128
PACK = 4
HALF = N // 2
L = P // 2
EARLY = 5 * T // 8
HV = V // 2
TURNED = 2


def tile_picked_gatedg_none_po_kernel(
    tc, x_words, x_scales, w1, w2, w3, offs, cen, pos1, pos2, pos3, out_0, out_1, out_2
):
    nc = tc.nc
    with ExitStack() as ctx:
        lists = ctx.enter_context(tc.tile_pool(name="lists", bufs=1))
        keep = ctx.enter_context(tc.tile_pool(name="keep", bufs=1))
        late = ctx.enter_context(tc.tile_pool(name="late", bufs=1))
        psum = ctx.enter_context(tc.psum_pool(name="psum", bufs=1))

        reused = {
            "yc2": 20480,
            "w3": 0, "gate0": 7168,
            "w2b": 12288, "rows_y2": 11264, "yc1": 13312, "yc3": 14336, "pre0": 15360,"pre1": 1024, "pre3": 4096, "gate_turned": 1024,
        }

        def place(shape, label, tag=None):
            if label in reused:
                return late.tile(shape, F32, name=label, offset=reused[label])
            return keep.tile(shape, F32, name=label, tag=tag or label, align_bytes=64)

        def load_list(name, src):
            tile = lists.tile([P, src.shape[1]], U16, name=name)
            nc.sync.dma_start(tile[:], src)
            return tile

        def load_half(name, w, half):
            raw_half = place([P, PACK, HALF], name)
            cols = slice(half * HALF, (half + 1) * HALF)
            nc.sync.dma_start(raw_half[:], w.rearrange("(p j) c -> p j c", j=PACK)[:, :, cols])
            return raw_half

        xs_all = keep.tile([P, T], U8, name="xs_all")
        nc.vector.memset(xs_all[:].bitcast(I32), 0)
        xw_all = keep.tile([P, T], U32, name="xw_all")

        def load_words(cols):
            words_in = x_words[0].rearrange("p n r -> p (n r)").bitcast(I32)
            nc.sync.dma_start(xw_all[:, cols].bitcast(I32), words_in[:, cols])

        def load_scales(queues):
            for q, queue in enumerate(queues):
                queue.dma_start(
                    xs_all[32 * q : 32 * q + 4, :].bitcast(I32), x_scales[0, 4 * q : 4 * q + 4, :].bitcast(I32)
                )

        raw = {}
        warm_in = keep.tile([P, 1], F32, name="warm_in", tag="identity")
        warm_out = keep.tile([P, 1], F32, name="warm_out")
        nc.vector.memset(warm_in[:], 0.0)
        load_words(slice(0, EARLY))
        offs_t = load_list("offs_t", offs)
        load_scales((nc.scalar, nc.scalar, nc.sync, nc.sync))
        nc.scalar.activation(warm_out[:], warm_in[:], SIGMOID)
        load_words(slice(EARLY, T))
        raw["y", 0] = load_half("w1a", w1, 0)
        raw["y", 1] = load_half("w1b", w1, 1)
        raw["e", 0] = load_half("w2a", w2, 0)
        cen_t = load_list("cen_t", cen)
        raw["e", 1] = load_half("w2b", w2, 1)
        pos_t = [load_list("pos0_t", pos1), load_list("pos1_t", pos2), load_list("pos2_t", pos3)]
        raw_h = place([P, PACK, N], "w3")
        nc.sync.dma_start(raw_h[:], w3.rearrange("(p j) c -> p j c", j=PACK))
        for half in range(2):
            raw["h", half] = raw_h[:, :, half * HALF : (half + 1) * HALF]

        identity = keep.tile([P, P], F32, name="identity", tag="identity")
        make_identity(nc, identity[:])

        xw = keep.tile([P, S], U32, name="xw", align_bytes=64)
        xs = keep.tile([P, S], U8, name="xs", align_bytes=64)

        grouped, codes, scales = {}, {}, {}
        for name in "yeh":
            if name == "h":
                grouped[name] = late.tile([P, 2 * PACK, L, PACK], BF16, name="grouped_h", offset=reused["yc2"], align_bytes=64)
            else:
                grouped[name] = keep.tile([P, 2 * PACK, L, PACK], BF16, name="grouped_" + name, align_bytes=64)
            codes[name] = keep.tile([P, N], U32, name="codes_" + name, align_bytes=64)
            scales[name] = keep.tile([P, N], U8, name="scales_" + name, align_bytes=64)

        def cast(name, half, first, last, runs, copy):
            copy(
                grouped[name][:, runs].rearrange("p t l j -> p l j t"),
                raw[name, half][:].rearrange("p j (l t) -> p l j t", t=PACK)[:, :, :, first:last],
            )

        def quantise(name, first, last, to):
            cols = slice(to * L, (to + last - first) * L)
            nc.vector.quantize_mx(
                out=codes[name][:, cols].bitcast(FP8X4),
                scales=scales[name][:, cols],
                in_=grouped[name][:, first:last].rearrange("p r l j -> p (r l j)"),
            )

        banks, rows = {}, {}

        def product(name, t, tag):
            cols = slice(t * P, (t + 1) * P)
            banks[name, t] = psum.tile([P, S], F32, name="bank_%s%d" % (name, t), tag=tag)
            nc.tensor.matmul_mx(
                out=banks[name, t][:],
                lhsT=codes[name][:, cols].bitcast(FP8X4),
                lhsT_scale=scales[name][:, cols],
                rhs=xw[:].bitcast(FP8X4),
                rhs_scale=xs[:],
                start=True,
                stop=True,
            )

        def empty(name, t, tag=None):
            rows[name, t] = place([P, S], "rows_%s%d" % (name, t), tag)
            nc.scalar.copy(rows[name, t][:], banks[name, t][:])

        yc, pre, gate, msg, turned = {}, {}, {}, {}, {}

        def fetch(dst, window, on_scalar_engine):
            if on_scalar_engine:
                nc.scalar.activation(dst, window, COPY)
            else:
                nc.vector.tensor_copy(dst, window)

        def centre(t, on_scalar_engine=True):
            yc[t] = place([P, V], "yc%d" % t)
            fetch(yc[t][:], rows["y", t][:].indirect(cen_t[:]), on_scalar_engine)

        def both_ends(t, first=0, last=3, label=None):
            part = place([P, last - first, V], label or "pre%d" % t)
            pre.setdefault(t, []).append((first, last, part))
            for d in range(first, last):
                nc.vector.tensor_tensor(part[:, d - first, :], rows["e", t][:].indirect(pos_t[d][:]), yc[t][:], ADD)

        def squash(t):
            gate[t] = place([P, 3, V], "gate%d" % t)
            for first, last, part in pre[t]:
                nc.scalar.activation(gate[t][:, first:last, :], part[:], SIGMOID)

        def passed_on(t, first=0, last=3):
            for d in range(first, last):
                msg[t, d] = place([P, V], "msg%d_%d" % (t, d))
                nc.vector.tensor_tensor(msg[t, d][:], rows["h", t][:].indirect(pos_t[d][:]), gate[t][:, d, :], MULT)

        z = keep.tile([P, PACK, V], F32, name="z")
        out_rows = out_0.rearrange("(p t) v -> p t v", t=PACK)
        held = {}

        def turn(t):
            turned[t] = psum.tile([P, 2, P], F32, name="turned%d" % t, tag="EB"[t])
            for half in range(2):
                for d in range(3):
                    nc.tensor.matmul(
                        turned[t][:, half, :], msg[t, d][:, half * P : (half + 1) * P], identity[:],
                        start=d == 0, stop=d == 2, is_transpose=True,
                    )

        def hold(t):
            if t == 0:
                held["sums"] = place([P, 2, 2, P], "held01", "rows_h2")
            nc.scalar.copy(
                held["sums"][:, :, :, t * L : (t + 1) * L], turned[t][:].rearrange("v h (u l) -> v h u l", u=2)
            )

        picked, sides = {}, {}

        def pick(name, d, on_scalar_engine=True):
            picked[name, d] = place([P, V], "picked_%s%d" % (name, d))
            fetch(picked[name, d][:], rows[name, TURNED][:].indirect(pos_t[d][:]), on_scalar_engine)

        def turn_both_ends():
            for half, tag in enumerate("HF"):
                cols = slice(half * P, (half + 1) * P)
                sides["pre", half] = psum.tile([P, 3, P], F32, name="pre_turned%d" % half, tag=tag)
                for d in range(3):
                    for src, first in ((yc[TURNED], True), (picked["e", d], False)):
                        nc.tensor.matmul(
                            sides["pre", half][:, d, :], src[:, cols], identity[:],
                            start=first, stop=not first, is_transpose=True,
                        )

        def squash_turned():
            gate[TURNED] = place([P, 2, 3, P], "gate_turned")
            for half in range(2):
                nc.scalar.activation(gate[TURNED][:, half], sides["pre", half][:], SIGMOID)

        def turn_passed_on():
            for half, tag in enumerate("GF"):
                sides["h", half] = psum.tile([P, 3, P], F32, name="h_turned%d" % half, tag=tag)
            for d in range(3):
                for half in range(2):
                    nc.tensor.transpose(
                        sides["h", half][:, d, :], picked["h", d][:, half * P : (half + 1) * P], identity[:]
                    )

        def weigh_turned(half):
            msg[TURNED, half] = place([P, 3, P], "msg_turned%d" % half)
            nc.vector.tensor_tensor(
                msg[TURNED, half][:].rearrange("v d (r l) -> v d r l", r=2),
                sides["h", half][:].rearrange("v d (r l) -> v d r l", r=2)[:, :, ::-1, :],
                gate[TURNED][:, half].rearrange("v d (r l) -> v d r l", r=2)[:, :, ::-1, :],
                MULT,
            )

        def back01():
            back = psum.tile([P, 2, 2, P], F32, name="back01", tag="H")
            for u in range(2):
                for half in range(2):
                    nc.tensor.transpose(back[:, u, half, :], held["sums"][:, half, u, :], identity[:])
            nc.scalar.copy(z[:, 0:2, :], back[:].rearrange("p u h v -> p u (h v)"))
            nc.sync.dma_start(out_rows[:, 0:2, :], z[:, 0:2, :])

        def back_turned():
            back = psum.tile([P, 2, P], F32, name="back_turned", tag="D")
            for half in range(2):
                for d in range(3):
                    nc.tensor.matmul(
                        back[:, half, :], msg[TURNED, half][:, d, :], identity[:],
                        start=d == 0, stop=d == 2, is_transpose=True,
                    )
            nc.scalar.copy(z[:, TURNED, :], back[:].rearrange("p h v -> p (h v)"))
            nc.sync.dma_start(out_rows[:, TURNED, :], z[:, TURNED, :])

        on_scalar, on_vector = nc.scalar.copy, nc.vector.tensor_copy
        nc.vector.tensor_copy(xs[:], xs_all[:].indirect(offs_t[:]))
        nc.vector.tensor_copy(xw[:], xw_all[:].indirect(offs_t[:]))
        cast("y", 0, 0, 2, slice(0, 2), on_scalar)
        quantise("y", 0, 2, 0)
        product("y", 0, "A")
        cast("y", 0, 2, 4, slice(5, 7), on_scalar)
        cast("y", 1, 0, 2, slice(2, 4), on_vector)
        cast("y", 1, 2, 4, slice(4, 8, 3), on_scalar)
        empty("y", 0)
        quantise("y", 2, 4, 2)
        product("y", 1, "C")
        quantise("y", 4, 8, 4)
        product("y", 3, "E")
        cast("e", 0, 0, 2, slice(0, 2), on_vector)
        cast("e", 0, 2, 4, slice(2, 4), on_vector)
        quantise("e", 0, 2, 0)
        product("e", 0, "B")
        quantise("e", 2, 4, 5)
        centre(0, False)
        empty("y", 1)
        cast("e", 1, 0, 2, slice(4, 6), on_vector)
        cast("e", 1, 2, 4, slice(6, 8), on_vector)
        quantise("e", 4, 6, 2)
        product("e", 1, "A")
        quantise("e", 6, 7, 4)
        quantise("e", 7, 8, 7)
        product("e", 2, "C")
        product("e", 3, "D")
        empty("y", 3)
        product("y", 2, "E")
        empty("e", 0)
        both_ends(0)
        centre(1)
        empty("y", 2)
        centre(3)
        empty("e", 1)
        empty("e", 2)
        empty("e", 3)
        pick("e", 0)
        pick("e", 1)
        pick("e", 2)
        cast("h", 0, 0, 4, slice(0, 4), on_vector)
        cast("h", 1, 0, 4, slice(4, 8), on_vector)
        quantise("h", 0, 2, 0)
        product("h", 0, "D")
        quantise("h", 2, 4, 5)
        quantise("h", 4, 6, 2)
        product("h", 1, "A")
        quantise("h", 6, 7, 4)
        quantise("h", 7, 8, 7)
        product("h", 2, "C")
        product("h", 3, "B")
        both_ends(1)
        both_ends(3)
        squash(0)
        empty("h", 0)
        centre(2)
        turn_both_ends()
        passed_on(0)
        empty("h", 1)
        empty("h", 2)
        pick("h", 2, False)
        squash(1)
        passed_on(1)
        squash_turned()
        pick("h", 0)
        pick("h", 1)
        turn_passed_on()
        weigh_turned(0)
        weigh_turned(1)
        empty("h", 3)
        squash(3)
        picked_last = place([P, V], "picked_last")
        fetch(picked_last[:], rows["h", 3][:].indirect(pos_t[0][:]), True)
        turn(0)
        hold(0)
        turn(1)
        hold(1)
        back_turned()
        back01()

        last = PACK - 1
        halves = [slice(0, HV), slice(HV, V)]
        part = keep.tile([P, V], F32, name="part")

        def first_add(half):
            cols = halves[half]
            nc.vector.tensor_tensor(part[:, cols], msg[last, 1][:, cols], msg[last, 2][:, cols], ADD)

        def second_add(half):
            cols = halves[half]
            nc.vector.tensor_tensor(z[:, last, cols], part[:, cols], msg[last, 0][:, cols], ADD)

        z_grouped = keep.tile([P, V, PACK], BF16, name="z_grouped", align_bytes=64)

        def group(cols, copy):
            copy(
                z_grouped[:, cols].rearrange("p (c i) t -> p c t i", i=2),
                z[:, :, cols].rearrange("p t (c i) -> p c t i", i=2),
            )

        z_codes = keep.tile([P, V], U32, name="z_codes", align_bytes=64)
        z_scales = keep.tile([P, V], U8, name="z_scales", align_bytes=64)
        words_out = out_1[0].rearrange("p v r -> p (v r)").bitcast(I32)

        def hand_on(half):
            nc.vector.quantize_mx(
                out=z_codes[:, halves[half]].bitcast(FP8X4),
                scales=z_scales[:, halves[half]],
                in_=z_grouped[:, halves[half]].rearrange("p v t -> p (v t)"),
            )

        passed_on(last, 1, 3)
        msg[last, 0] = place([P, V], "msg_last")
        nc.vector.tensor_tensor(msg[last, 0][:], picked_last[:], gate[last][:, 0, :], MULT)
        first_add(1)
        first_add(0)
        second_add(1)
        second_add(0)
        nc.sync.dma_start(out_rows[:, last, :], z[:, last, :])
        group(halves[1], nc.vector.tensor_copy)
        group(slice(0, HV // 2), nc.scalar.copy)
        group(slice(HV // 2, HV), nc.vector.tensor_copy)
        hand_on(1)
        hand_on(0)
        nc.sync.dma_start(words_out, z_codes[:].bitcast(I32))
        for q in range(4):
            queue = nc.sync if q % 2 == 1 else nc.scalar
            queue.dma_start(
                out_2[0, 4 * q : 4 * q + 4, :].bitcast(I32), z_scales[32 * q : 32 * q + 4, :].bitcast(I32)
            )
